import numpy as np
import ml_dtypes


def mxq(x, axis, fmt="e4m3"):
    dtype, down = {"e4m3": (ml_dtypes.float8_e4m3fn, 7), "e5m2": (ml_dtypes.float8_e5m2, 14)}[fmt]
    v = np.moveaxis(np.asarray(x, np.float32).astype(ml_dtypes.bfloat16).astype(np.float64), axis, -1)
    blocks = v.reshape(v.shape[:-1] + (-1, 32))
    amax = np.abs(blocks).max(-1, keepdims=True)
    byte = np.maximum(np.where(amax > 0, np.frexp(amax)[1] - 1 + 127, 0) - down, 1)
    scale = np.exp2(byte - 127.0)
    codes = (blocks / scale).astype(np.float32).astype(dtype).astype(np.float64)
    return np.moveaxis((codes * scale).reshape(v.shape), -1, axis)


WIDE = False


def mx_kscale(k):
    if not WIDE:
        return np.ones(k)
    levels = np.array([10, -10, 5, -5, 0])
    if k % 512:
        return np.exp2(np.random.permutation(np.resize(levels, k // 32))).repeat(32)
    a = np.empty((k // 512, 16))
    for p in range(k // 512):
        a[p, :8] = np.random.permutation(np.resize(levels, 8))
        for g in range(8):
            far = levels[np.abs(levels - a[p, g]) >= 10]
            a[p, g + 8] = far[np.random.randint(len(far))]
    return np.exp2(a.ravel()).repeat(32)


BF16 = ml_dtypes.bfloat16


def bf(x):
    return np.asarray(x, np.float32).astype(BF16)


def f64(x):
    return np.asarray(x).astype(np.float64)

def planes(Y):
    n, m = Y.shape
    b = f64(bf(Y)).reshape(n // 32, 32, m)
    amax = np.abs(b).max(1)
    byte = np.clip(np.where(amax > 0, np.frexp(amax)[1] - 1 + 127 - 7, 1), 1, 254)
    codes = (b * np.exp2(127.0 - byte)[:, None, :]).reshape(n, m).astype(np.float32).astype(ml_dtypes.float8_e4m3fn).view(np.uint8)
    words = codes.reshape(n // 512, 128, 4, m).transpose(0, 1, 3, 2)
    return np.ascontiguousarray(words), np.ascontiguousarray(byte.astype(np.uint8).reshape(n // 512, 16, m))


B, T, S, D, N = 2, 512, 1536, 1024, 1024

SHARP = 2.0
VALUE_STD = 3.0


def setup_inputs():
    s = mx_kscale(S)
    r = mx_kscale(D)
    logits = SHARP * np.random.randn(B, T, S)
    e = np.exp(logits - logits.max(axis=-1, keepdims=True))
    weights = e / e.sum(axis=-1, keepdims=True)
    spread = np.exp(0.8 * np.random.randn(N))
    values = VALUE_STD * np.random.randn(B, S, N) * spread
    return {
        "mix": bf(weights * s),
        "values": bf(values / s[:, None]),
        "x": bf(np.random.randn(B, T, D) * r),
        "w_gate": bf(np.random.randn(D, N) / np.sqrt(D) / r[:, None]),
        "b_gate": bf(0.5 * np.random.randn(N)),
    }


def reference(mix, values, x, w_gate, b_gate):
    mix_q = mxq(f64(mix), 2, "e4m3")
    values_q = mxq(f64(values), 1, "e4m3")
    context = mix_q @ values_q
    x_q = mxq(f64(x), 2, "e4m3")
    w_q = mxq(f64(w_gate), 0, "e4m3")
    pre = x_q @ w_q
    y = context * np.tanh(pre + f64(b_gate))
    words, scales = planes(y.reshape(B * T, N).T)
    return y, words, scales

@@ -1,0 +1,443 @@
+from contextlib import ExitStack
+
+import concourse.mybir as mybir
+from concourse.masks import make_identity
+
+B, T, S, D, N = 2, 512, 1536, 1024, 1024
+FLOPS = 2 * B * T * N * (S + D)
+
+F32 = mybir.dt.float32
+BF16 = mybir.dt.bfloat16
+U32 = mybir.dt.uint32
+I32 = mybir.dt.int32
+U8 = mybir.dt.uint8
+FP8X4 = mybir.dt.float8_e4m3fn_x4
+TANH = mybir.ActivationFunctionType.Tanh
+MULT = mybir.AluOpType.mult
+
+P = 128
+PACK = 4
+K_PASS = P * PACK
+GROUP = 512
+HALF = 256
+PAIRS = 64
+
+
+def tile_gated_cross_value_mix_g1_kernel(tc, mix, values, x, w_gate, b_gate, out_0, out_1, out_2):
+    nc = tc.nc
+    with ExitStack() as ctx:
+        sb = ctx.enter_context(tc.tile_pool(name="sb", bufs=1))
+        psum = ctx.enter_context(tc.psum_pool(name="psum", bufs=8))
+        ctx.enter_context(tc.manual_schedule())
+
+        on_vector = nc.vector.tensor_copy
+        on_scalar = nc.scalar.copy
+        raw = {}
+        staged = {}
+        codes = {}
+        scales = {}
+        gated = {}
+        banks = {}
+        rows_out = {}
+
+        def new_bank(name):
+            return psum.tile([P, GROUP], F32, name=name, bufs=4)
+
+        def operand(key):
+            if key not in codes:
+                codes[key] = sb.tile([P, GROUP], U32, name="codes", bufs=22, align_bytes=64)
+                scales[key] = sb.tile([P, GROUP], U8, name="scales", bufs=22, align_bytes=64)
+            return codes[key], scales[key]
+
+        def load_rows(key, src):
+            tile = sb.tile([P, PACK, GROUP], BF16, name="raw", bufs=10)
+            nc.sync.dma_start(out=tile[:], in_=src.rearrange("(p j) n -> p j n", j=PACK))
+            raw[key] = tile[:]
+
+        def load_w(g, c):
+            load_rows(("w", g, c), w_gate[K_PASS * c : K_PASS * (c + 1), GROUP * g : GROUP * (g + 1)])
+
+        def load_v(b, g, c):
+            load_rows(("v", b, g, c), values[b, K_PASS * c : K_PASS * (c + 1), GROUP * g : GROUP * (g + 1)])
+
+        def load_v_wide(b, c):
+            tile = sb.tile([P, PACK, N], BF16, name="raw_wide", bufs=3)
+            src = values[b, K_PASS * c : K_PASS * (c + 1), :]
+            nc.sync.dma_start(out=tile[:], in_=src.rearrange("(p j) n -> p j n", j=PACK))
+            for g in range(2):
+                raw[("v", b, g, c)] = tile[:, :, GROUP * g : GROUP * (g + 1)]
+
+        def load_x(b, h):
+            tile = sb.tile([P, 2, D], BF16, name="raw", bufs=10)
+            nc.sync.dma_start(out=tile[:], in_=x[b, HALF * h : HALF * (h + 1), :].rearrange("(j p) k -> p j k", p=P))
+            raw[("x", b, h)] = tile[:]
+
+        def load_mix(b, h):
+            tile = sb.tile([P, 2, S], BF16, name="raw_mix", bufs=3)
+            nc.sync.dma_start(out=tile[:], in_=mix[b, HALF * h : HALF * (h + 1), :].rearrange("(j p) k -> p j k", p=P))
+            raw[("mix", b, h)] = tile[:]
+
+        def staging(key):
+            if key not in staged:
+                staged[key] = sb.tile([P, PACK * GROUP], BF16, name="staged", bufs=4, align_bytes=64)
+            return staged[key]
+
+        def interleave(copy, key, lo, hi):
+            dst = staging(key)[:].rearrange("p (t a m j) -> p a t m j", t=PACK, m=2, j=PACK)
+            src = raw[key].rearrange("p j (a m t) -> p a t m j", m=2, t=PACK)
+            copy(out=dst[:, lo:hi], in_=src[:, lo:hi])
+
+        def quantize_rows(key):
+            cd, sc = operand(key)
+            nc.vector.quantize_mx(out=cd[:].bitcast(FP8X4), scales=sc[:], in_=staged[key][:])
+
+        def turn(name, b, h, c):
+            words = raw[(name, b, h)].bitcast(F32)
+            bank = new_bank("bank")
+            banks[(name, b, h, c)] = bank
+            for j in range(2):
+                for u in range(2):
+                    slot = 2 * j + u
+                    nc.tensor.transpose(
+                        bank[:, P * slot : P * (slot + 1)], words[:, j, 256 * c + u : 256 * (c + 1) : 2], ident[:]
+                    )
+
+        def collect(name, b, h, c):
+            bank = banks[(name, b, h, c)]
+            tile = sb.tile([P, PACK * HALF], BF16, name="staged_tokens", bufs=6, align_bytes=64)
+            staged[(name, b, h, c)] = tile
+            nc.scalar.copy(
+                out=tile[:].bitcast(F32).rearrange("p (j r u) -> p j r u", j=2, u=2),
+                in_=bank[:].rearrange("p (j u r) -> p j r u", j=2, u=2),
+            )
+
+        def quantize_tokens(name, b, h, c):
+            cd, sc = operand((name, b, c))
+            cols = slice(HALF * h, HALF * (h + 1))
+            nc.vector.quantize_mx(out=cd[:, cols].bitcast(FP8X4), scales=sc[:, cols], in_=staged[(name, b, h, c)][:])
+
+        def product(name, stationary, moving, t):
+            bank = new_bank(name)
+            cols = slice(P * t, P * (t + 1))
+            for c in range(len(moving)):
+                nc.tensor.matmul_mx(
+                    out=bank[:],
+                    lhsT=codes[stationary[c]][:, cols].bitcast(FP8X4),
+                    lhsT_scale=scales[stationary[c]][:, cols],
+                    rhs=codes[moving[c]][:].bitcast(FP8X4),
+                    rhs_scale=scales[moving[c]][:],
+                    start=(c == 0),
+                    stop=(c == len(moving) - 1),
+                )
+            return bank
+
+        def pre(b, g, t):
+            banks[("pre", b, g, t)] = product("bank", [("w", g, c) for c in range(2)], [("x", b, c) for c in range(2)], t)
+
+        def gate(b, g, t):
+            if (b, g) not in gated:
+                gated[(b, g)] = sb.tile([P, PACK, T], F32, name="gated", bufs=4)
+            bank = banks[("pre", b, g, t)]
+            nc.scalar.activation(out=gated[(b, g)][:, t, :], in_=bank[:], func=TANH, bias=bias[:, g, t : t + 1])
+
+        def context(b, g, t):
+            banks[(b, g, t)] = product("acc", [("v", b, g, c) for c in range(3)], [("mix", b, c) for c in range(3)], t)
+
+        def multiply(b, g, t):
+            y_t = gated[(b, g)][:, t, :]
+            nc.vector.tensor_tensor(out=y_t, in0=banks[(b, g, t)][:], in1=y_t, op=MULT)
+
+        def turn_back(b, g, j):
+            bank = new_bank("bank")
+            banks[("back", b, g, j)] = bank
+            for t in range(PACK):
+                nc.tensor.transpose(bank[:, P * t : P * (t + 1)], gated[(b, g)][:, t, P * j : P * (j + 1)], ident[:])
+
+        def collect_rows(copy, b, g, j):
+            bank = banks[("back", b, g, j)]
+            tile = sb.tile([P, GROUP], F32, name="rows_out", bufs=8)
+            copy(out=tile[:].rearrange("p (m t) -> p m t", t=PACK), in_=bank[:].rearrange("p (t m) -> p m t", t=PACK))
+            rows_out[(b, g, j)] = tile
+
+        def store_rows(b, g, j):
+            nc.sync.dma_start(out=out_0[b, P * j : P * (j + 1), GROUP * g : GROUP * (g + 1)], in_=rows_out[(b, g, j)][:])
+
+        def round_result(copy, b, g, lo, hi):
+            if ("y", b, g) not in staged:
+                staged[("y", b, g)] = sb.tile([P, PACK * GROUP], BF16, name="rounded", bufs=2, align_bytes=64)
+            dst = staged[("y", b, g)][:].rearrange("p (a i t) -> p a t i", i=4, t=PACK)
+            src = gated[(b, g)][:].rearrange("p t (a i) -> p a t i", i=4)
+            copy(out=dst[:, 2 * lo : 2 * hi], in_=src[:, 2 * lo : 2 * hi])
+
+        def quantize_result(b, g):
+            y_codes = sb.tile([P, T], U32, name="y_codes", bufs=4, align_bytes=64)
+            cols = slice(T * b, T * (b + 1))
+            nc.vector.quantize_mx(out=y_codes[:].bitcast(FP8X4), scales=y_scales[:, g, cols], in_=staged[("y", b, g)][:])
+            codes[("y", b, g)] = y_codes
+
+        def store_words(b, g):
+            dst = out_1[g].rearrange("p m t -> p (m t)").bitcast(I32)
+            nc.sync.dma_start(out=dst[:, T * b : T * (b + 1)], in_=codes[("y", b, g)][:].bitcast(I32))
+
+        ident = sb.tile([P, P], F32, name="ident")
+        make_identity(nc, ident[:])
+        bias = sb.tile([P, 2, PACK], BF16, name="bias")
+        y_scales = sb.tile([P, 2, B * T], U8, name="y_scales", align_bytes=64)
+        warm = sb.tile([P, 2], F32, name="warm")
+        nc.gpsimd.memset(warm[:, 0:1], 0.0)
+        nc.scalar.activation(out=warm[:, 1:2], in_=warm[:, 0:1], func=TANH)
+
+        load_w(0, 0)
+        load_x(0, 0)
+        load_w(0, 1)
+        load_x(0, 1)
+        nc.sync.dma_start(out=bias[:], in_=b_gate.rearrange("(g p t) -> p g t", g=2, t=PACK))
+        load_w(1, 0)
+        load_x(1, 0)
+        load_w(1, 1)
+        load_x(1, 1)
+        load_mix(0, 0)
+        load_v(0, 0, 0)
+        load_mix(0, 1)
+        load_v(0, 0, 1)
+        interleave(on_scalar, ("w", 0, 0), 32, 64)
+        interleave(on_vector, ("w", 0, 0), 0, 32)
+        load_v(0, 0, 2)
+        quantize_rows(("w", 0, 0))
+        interleave(on_vector, ("w", 0, 1), 0, 64)
+        turn("x", 0, 0, 0)
+        collect("x", 0, 0, 0)
+        quantize_tokens("x", 0, 0, 0)
+        turn("x", 0, 0, 1)
+        load_v(0, 1, 0)
+        load_v(0, 1, 1)
+        collect("x", 0, 0, 1)
+        quantize_tokens("x", 0, 0, 1)
+        quantize_rows(("w", 0, 1))
+        interleave(on_vector, ("w", 1, 0), 0, 32)
+        turn("x", 0, 1, 0)
+        collect("x", 0, 1, 0)
+        quantize_tokens("x", 0, 1, 0)
+        turn("x", 0, 1, 1)
+        load_v(0, 1, 2)
+        load_mix(1, 0)
+        collect("x", 0, 1, 1)
+        interleave(on_scalar, ("w", 1, 0), 32, 64)
+        quantize_tokens("x", 0, 1, 1)
+        quantize_rows(("w", 1, 0))
+        interleave(on_vector, ("w", 1, 1), 0, 64)
+        turn("x", 1, 0, 0)
+        collect("x", 1, 0, 0)
+        quantize_tokens("x", 1, 0, 0)
+        turn("x", 1, 0, 1)
+        collect("x", 1, 0, 1)
+        quantize_tokens("x", 1, 0, 1)
+        quantize_rows(("w", 1, 1))
+        interleave(on_vector, ("v", 0, 0, 0), 0, 64)
+        pre(0, 0, 0)
+        gate(0, 0, 0)
+        pre(0, 0, 1)
+        gate(0, 0, 1)
+        pre(0, 0, 2)
+        gate(0, 0, 2)
+        pre(0, 0, 3)
+        gate(0, 0, 3)
+        turn("x", 1, 1, 0)
+        collect("x", 1, 1, 0)
+        quantize_tokens("x", 1, 1, 0)
+        turn("x", 1, 1, 1)
+        collect("x", 1, 1, 1)
+        quantize_tokens("x", 1, 1, 1)
+        quantize_rows(("v", 0, 0, 0))
+        interleave(on_vector, ("v", 0, 0, 1), 0, 64)
+        pre(0, 1, 0)
+        gate(0, 1, 0)
+        pre(0, 1, 1)
+        gate(0, 1, 1)
+        pre(0, 1, 2)
+        gate(0, 1, 2)
+        pre(0, 1, 3)
+        gate(0, 1, 3)
+        turn("mix", 0, 0, 0)
+        collect("mix", 0, 0, 0)
+        quantize_tokens("mix", 0, 0, 0)
+        turn("mix", 0, 0, 1)
+        collect("mix", 0, 0, 1)
+        quantize_tokens("mix", 0, 0, 1)
+        turn("mix", 0, 0, 2)
+        load_mix(1, 1)
+        load_v_wide(1, 0)
+        load_v_wide(1, 1)
+        load_v_wide(1, 2)
+        collect("mix", 0, 0, 2)
+        quantize_tokens("mix", 0, 0, 2)
+        quantize_rows(("v", 0, 0, 1))
+        interleave(on_vector, ("v", 0, 0, 2), 0, 64)
+        turn("mix", 0, 1, 0)
+        collect("mix", 0, 1, 0)
+        quantize_tokens("mix", 0, 1, 0)
+        turn("mix", 0, 1, 1)
+        collect("mix", 0, 1, 1)
+        quantize_tokens("mix", 0, 1, 1)
+        turn("mix", 0, 1, 2)
+        collect("mix", 0, 1, 2)
+        quantize_tokens("mix", 0, 1, 2)
+        quantize_rows(("v", 0, 0, 2))
+        interleave(on_vector, ("v", 0, 1, 0), 0, 32)
+        interleave(on_vector, ("v", 0, 1, 1), 0, 32)
+        pre(1, 0, 0)
+        gate(1, 0, 0)
+        pre(1, 0, 1)
+        gate(1, 0, 1)
+        pre(1, 0, 2)
+        gate(1, 0, 2)
+        pre(1, 0, 3)
+        gate(1, 0, 3)
+        interleave(on_scalar, ("v", 0, 1, 0), 32, 64)
+        interleave(on_scalar, ("v", 0, 1, 1), 32, 64)
+        interleave(on_scalar, ("v", 0, 1, 2), 32, 64)
+        quantize_rows(("v", 0, 1, 0))
+        interleave(on_vector, ("v", 0, 1, 2), 0, 32)
+        context(0, 0, 0)
+        multiply(0, 0, 0)
+        context(0, 0, 1)
+        multiply(0, 0, 1)
+        quantize_rows(("v", 0, 1, 1))
+        context(0, 0, 2)
+        multiply(0, 0, 2)
+        context(0, 0, 3)
+        multiply(0, 0, 3)
+        quantize_rows(("v", 0, 1, 2))
+        turn("mix", 1, 0, 0)
+        collect("mix", 1, 0, 0)
+        quantize_tokens("mix", 1, 0, 0)
+        turn("mix", 1, 0, 1)
+        collect("mix", 1, 0, 1)
+        quantize_tokens("mix", 1, 0, 1)
+        turn("mix", 1, 0, 2)
+        collect("mix", 1, 0, 2)
+        quantize_tokens("mix", 1, 0, 2)
+        interleave(on_vector, ("v", 1, 0, 0), 0, 32)
+        turn("mix", 1, 1, 0)
+        collect("mix", 1, 1, 0)
+        quantize_tokens("mix", 1, 1, 0)
+        turn("mix", 1, 1, 1)
+        collect("mix", 1, 1, 1)
+        quantize_tokens("mix", 1, 1, 1)
+        turn("mix", 1, 1, 2)
+        collect("mix", 1, 1, 2)
+        interleave(on_scalar, ("v", 1, 0, 0), 32, 64)
+        interleave(on_scalar, ("v", 1, 0, 1), 32, 64)
+        interleave(on_scalar, ("v", 1, 0, 2), 32, 64)
+        quantize_tokens("mix", 1, 1, 2)
+        interleave(on_vector, ("v", 1, 0, 1), 0, 32)
+        quantize_rows(("v", 1, 0, 0))
+        context(0, 1, 0)
+        multiply(0, 1, 0)
+        context(0, 1, 1)
+        multiply(0, 1, 1)
+        quantize_rows(("v", 1, 0, 1))
+        context(0, 1, 2)
+        multiply(0, 1, 2)
+        context(0, 1, 3)
+        multiply(0, 1, 3)
+        interleave(on_vector, ("v", 1, 0, 2), 0, 32)
+        interleave(on_vector, ("v", 1, 1, 0), 0, 48)
+        quantize_rows(("v", 1, 0, 2))
+        interleave(on_vector, ("v", 1, 1, 1), 0, 48)
+        turn_back(0, 0, 0)
+        collect_rows(on_scalar, 0, 0, 0)
+        store_rows(0, 0, 0)
+        turn_back(0, 0, 1)
+        collect_rows(on_scalar, 0, 0, 1)
+        store_rows(0, 0, 1)
+        turn_back(0, 0, 2)
+        collect_rows(on_scalar, 0, 0, 2)
+        store_rows(0, 0, 2)
+        turn_back(0, 0, 3)
+        collect_rows(on_scalar, 0, 0, 3)
+        store_rows(0, 0, 3)
+        interleave(on_scalar, ("v", 1, 1, 0), 48, 64)
+        quantize_rows(("v", 1, 1, 0))
+        interleave(on_vector, ("v", 1, 1, 2), 0, 48)
+        turn_back(0, 1, 0)
+        collect_rows(on_scalar, 0, 1, 0)
+        store_rows(0, 1, 0)
+        turn_back(0, 1, 1)
+        collect_rows(on_scalar, 0, 1, 1)
+        store_rows(0, 1, 1)
+        turn_back(0, 1, 2)
+        collect_rows(on_scalar, 0, 1, 2)
+        store_rows(0, 1, 2)
+        turn_back(0, 1, 3)
+        collect_rows(on_scalar, 0, 1, 3)
+        store_rows(0, 1, 3)
+        interleave(on_scalar, ("v", 1, 1, 1), 48, 64)
+        interleave(on_scalar, ("v", 1, 1, 2), 48, 64)
+        round_result(on_scalar, 0, 0, 0, 64)
+        quantize_rows(("v", 1, 1, 1))
+        context(1, 0, 0)
+        multiply(1, 0, 0)
+        quantize_rows(("v", 1, 1, 2))
+        context(1, 0, 1)
+        multiply(1, 0, 1)
+        context(1, 0, 2)
+        multiply(1, 0, 2)
+        context(1, 0, 3)
+        multiply(1, 0, 3)
+        quantize_result(0, 0)
+        store_words(0, 0)
+        round_result(on_vector, 0, 1, 0, 64)
+        pre(1, 1, 0)
+        gate(1, 1, 0)
+        pre(1, 1, 1)
+        gate(1, 1, 1)
+        pre(1, 1, 2)
+        gate(1, 1, 2)
+        pre(1, 1, 3)
+        gate(1, 1, 3)
+        context(1, 1, 0)
+        multiply(1, 1, 0)
+        context(1, 1, 1)
+        multiply(1, 1, 1)
+        quantize_result(0, 1)
+        round_result(on_vector, 1, 0, 0, 16)
+        turn_back(1, 0, 0)
+        collect_rows(on_scalar, 1, 0, 0)
+        store_rows(1, 0, 0)
+        turn_back(1, 0, 1)
+        collect_rows(on_scalar, 1, 0, 1)
+        store_rows(1, 0, 1)
+        turn_back(1, 0, 2)
+        collect_rows(on_scalar, 1, 0, 2)
+        store_rows(1, 0, 2)
+        store_words(0, 1)
+        turn_back(1, 0, 3)
+        collect_rows(on_scalar, 1, 0, 3)
+        store_rows(1, 0, 3)
+        round_result(on_scalar, 1, 0, 16, 64)
+        context(1, 1, 2)
+        multiply(1, 1, 2)
+        context(1, 1, 3)
+        multiply(1, 1, 3)
+        round_result(on_vector, 1, 1, 0, 64)
+        quantize_result(1, 0)
+        quantize_result(1, 1)
+        turn_back(1, 1, 0)
+        collect_rows(on_scalar, 1, 1, 0)
+        store_rows(1, 1, 0)
+        turn_back(1, 1, 1)
+        collect_rows(on_scalar, 1, 1, 1)
+        store_rows(1, 1, 1)
+        store_words(1, 0)
+        turn_back(1, 1, 2)
+        collect_rows(on_scalar, 1, 1, 2)
+        store_rows(1, 1, 2)
+        store_words(1, 1)
+        turn_back(1, 1, 3)
+        collect_rows(on_scalar, 1, 1, 3)
+        store_rows(1, 1, 3)
+
+        for q in range(4):
+            dst = out_2[:, 4 * q : 4 * (q + 1), :].rearrange("g r m -> r g m")
+            nc.sync.dma_start(out=dst.bitcast(I32), in_=y_scales[32 * q : 32 * q + 4, :, :].bitcast(I32))

@@ -79,7 +79,7 @@ def tile_gated_cross_value_mix_g1_kernel(tc, mix, values, x, w_gate, b_gate, out
 
         def staging(key):
             if key not in staged:
-                staged[key] = sb.tile([P, PACK * GROUP], BF16, name="staged", bufs=4, align_bytes=64)
+                staged[key] = sb.tile([P, PACK * GROUP], BF16, name="staged", bufs=5, align_bytes=64)
             return staged[key]
 
         def interleave(copy, key, lo, hi):
@@ -143,6 +143,35 @@ def tile_gated_cross_value_mix_g1_kernel(tc, mix, values, x, w_gate, b_gate, out
         def context(b, g, t):
             banks[(b, g, t)] = product("acc", [("v", b, g, c) for c in range(3)], [("mix", b, c) for c in range(3)], t)
 
+        def context_pass(b, g, c):
+            for t in range(PACK):
+                if c == 0:
+                    banks[(b, g, t)] = new_bank("acc")
+                cols = slice(P * t, P * (t + 1))
+                nc.tensor.matmul_mx(
+                    out=banks[(b, g, t)][:],
+                    lhsT=codes[("v", b, g, c)][:, cols].bitcast(FP8X4),
+                    lhsT_scale=scales[("v", b, g, c)][:, cols],
+                    rhs=codes[("mix", b, c)][:].bitcast(FP8X4),
+                    rhs_scale=scales[("mix", b, c)][:],
+                    start=(c == 0),
+                    stop=(c == 2),
+                )
+
+        def warm_up(n):
+            bank = new_bank("acc")
+            key = ("w", 0, 0)
+            for i in range(n):
+                nc.tensor.matmul_mx(
+                    out=bank[:],
+                    lhsT=codes[key][:, :P].bitcast(FP8X4),
+                    lhsT_scale=scales[key][:, :P],
+                    rhs=codes[key][:].bitcast(FP8X4),
+                    rhs_scale=scales[key][:],
+                    start=True,
+                    stop=True,
+                )
+
         def multiply(b, g, t):
             y_t = gated[(b, g)][:, t, :]
             nc.vector.tensor_tensor(out=y_t, in0=banks[(b, g, t)][:], in1=y_t, op=MULT)
@@ -191,18 +220,17 @@ def tile_gated_cross_value_mix_g1_kernel(tc, mix, values, x, w_gate, b_gate, out
         load_x(0, 0)
         load_w(0, 1)
         load_x(0, 1)
-        nc.sync.dma_start(out=bias[:], in_=b_gate.rearrange("(g p t) -> p g t", g=2, t=PACK))
         load_w(1, 0)
         load_x(1, 0)
         load_w(1, 1)
+        nc.sync.dma_start(out=bias[:], in_=b_gate.rearrange("(g p t) -> p g t", g=2, t=PACK))
         load_x(1, 1)
-        load_mix(0, 0)
         load_v(0, 0, 0)
-        load_mix(0, 1)
         load_v(0, 0, 1)
-        interleave(on_scalar, ("w", 0, 0), 32, 64)
-        interleave(on_vector, ("w", 0, 0), 0, 32)
+        load_mix(0, 0)
+        interleave(on_vector, ("w", 0, 0), 0, 64)
         load_v(0, 0, 2)
+        load_mix(0, 1)
         quantize_rows(("w", 0, 0))
         interleave(on_vector, ("w", 0, 1), 0, 64)
         turn("x", 0, 0, 0)
@@ -214,7 +242,8 @@ def tile_gated_cross_value_mix_g1_kernel(tc, mix, values, x, w_gate, b_gate, out
         collect("x", 0, 0, 1)
         quantize_tokens("x", 0, 0, 1)
         quantize_rows(("w", 0, 1))
-        interleave(on_vector, ("w", 1, 0), 0, 32)
+        interleave(on_vector, ("w", 1, 0), 0, 48)
+        warm_up(2)
         turn("x", 0, 1, 0)
         collect("x", 0, 1, 0)
         quantize_tokens("x", 0, 1, 0)
@@ -222,10 +251,11 @@ def tile_gated_cross_value_mix_g1_kernel(tc, mix, values, x, w_gate, b_gate, out
         load_v(0, 1, 2)
         load_mix(1, 0)
         collect("x", 0, 1, 1)
-        interleave(on_scalar, ("w", 1, 0), 32, 64)
+        interleave(on_scalar, ("w", 1, 0), 48, 64)
         quantize_tokens("x", 0, 1, 1)
-        quantize_rows(("w", 1, 0))
         interleave(on_vector, ("w", 1, 1), 0, 64)
+        quantize_rows(("w", 1, 0))
+        warm_up(2)
         turn("x", 1, 0, 0)
         collect("x", 1, 0, 0)
         quantize_tokens("x", 1, 0, 0)
@@ -234,6 +264,7 @@ def tile_gated_cross_value_mix_g1_kernel(tc, mix, values, x, w_gate, b_gate, out
         quantize_tokens("x", 1, 0, 1)
         quantize_rows(("w", 1, 1))
         interleave(on_vector, ("v", 0, 0, 0), 0, 64)
+        interleave(on_vector, ("v", 0, 0, 1), 0, 64)
         pre(0, 0, 0)
         gate(0, 0, 0)
         pre(0, 0, 1)
@@ -249,21 +280,22 @@ def tile_gated_cross_value_mix_g1_kernel(tc, mix, values, x, w_gate, b_gate, out
         collect("x", 1, 1, 1)
         quantize_tokens("x", 1, 1, 1)
         quantize_rows(("v", 0, 0, 0))
-        interleave(on_vector, ("v", 0, 0, 1), 0, 64)
+        interleave(on_vector, ("v", 0, 0, 2), 0, 64)
+        quantize_rows(("v", 0, 0, 1))
         pre(0, 1, 0)
         gate(0, 1, 0)
         pre(0, 1, 1)
         gate(0, 1, 1)
-        pre(0, 1, 2)
-        gate(0, 1, 2)
-        pre(0, 1, 3)
-        gate(0, 1, 3)
         turn("mix", 0, 0, 0)
         collect("mix", 0, 0, 0)
         quantize_tokens("mix", 0, 0, 0)
         turn("mix", 0, 0, 1)
         collect("mix", 0, 0, 1)
         quantize_tokens("mix", 0, 0, 1)
+        pre(0, 1, 2)
+        gate(0, 1, 2)
+        pre(0, 1, 3)
+        gate(0, 1, 3)
         turn("mix", 0, 0, 2)
         load_mix(1, 1)
         load_v_wide(1, 0)
@@ -271,155 +303,148 @@ def tile_gated_cross_value_mix_g1_kernel(tc, mix, values, x, w_gate, b_gate, out
         load_v_wide(1, 2)
         collect("mix", 0, 0, 2)
         quantize_tokens("mix", 0, 0, 2)
-        quantize_rows(("v", 0, 0, 1))
-        interleave(on_vector, ("v", 0, 0, 2), 0, 64)
+        quantize_rows(("v", 0, 0, 2))
+        interleave(on_vector, ("v", 0, 1, 0), 0, 64)
         turn("mix", 0, 1, 0)
         collect("mix", 0, 1, 0)
         quantize_tokens("mix", 0, 1, 0)
+        pre(1, 0, 0)
+        gate(1, 0, 0)
+        pre(1, 0, 1)
+        gate(1, 0, 1)
         turn("mix", 0, 1, 1)
         collect("mix", 0, 1, 1)
         quantize_tokens("mix", 0, 1, 1)
         turn("mix", 0, 1, 2)
         collect("mix", 0, 1, 2)
         quantize_tokens("mix", 0, 1, 2)
-        quantize_rows(("v", 0, 0, 2))
-        interleave(on_vector, ("v", 0, 1, 0), 0, 32)
-        interleave(on_vector, ("v", 0, 1, 1), 0, 32)
-        pre(1, 0, 0)
-        gate(1, 0, 0)
-        pre(1, 0, 1)
-        gate(1, 0, 1)
+        interleave(on_vector, ("v", 0, 1, 2), 0, 64)
+        quantize_rows(("v", 0, 1, 0))
         pre(1, 0, 2)
         gate(1, 0, 2)
         pre(1, 0, 3)
         gate(1, 0, 3)
-        interleave(on_scalar, ("v", 0, 1, 0), 32, 64)
-        interleave(on_scalar, ("v", 0, 1, 1), 32, 64)
-        interleave(on_scalar, ("v", 0, 1, 2), 32, 64)
-        quantize_rows(("v", 0, 1, 0))
-        interleave(on_vector, ("v", 0, 1, 2), 0, 32)
+        interleave(on_scalar, ("v", 0, 1, 1), 0, 64)
         context(0, 0, 0)
         multiply(0, 0, 0)
         context(0, 0, 1)
         multiply(0, 0, 1)
-        quantize_rows(("v", 0, 1, 1))
-        context(0, 0, 2)
-        multiply(0, 0, 2)
-        context(0, 0, 3)
-        multiply(0, 0, 3)
         quantize_rows(("v", 0, 1, 2))
+        quantize_rows(("v", 0, 1, 1))
         turn("mix", 1, 0, 0)
         collect("mix", 1, 0, 0)
-        quantize_tokens("mix", 1, 0, 0)
         turn("mix", 1, 0, 1)
         collect("mix", 1, 0, 1)
-        quantize_tokens("mix", 1, 0, 1)
+        context(0, 0, 2)
+        multiply(0, 0, 2)
         turn("mix", 1, 0, 2)
         collect("mix", 1, 0, 2)
-        quantize_tokens("mix", 1, 0, 2)
-        interleave(on_vector, ("v", 1, 0, 0), 0, 32)
         turn("mix", 1, 1, 0)
         collect("mix", 1, 1, 0)
-        quantize_tokens("mix", 1, 1, 0)
+        interleave(on_scalar, ("v", 1, 0, 0), 0, 64)
+        context(0, 0, 3)
+        multiply(0, 0, 3)
+        interleave(on_vector, ("v", 1, 0, 1), 0, 64)
+        quantize_tokens("mix", 1, 0, 0)
+        quantize_tokens("mix", 1, 0, 1)
+        quantize_tokens("mix", 1, 0, 2)
         turn("mix", 1, 1, 1)
         collect("mix", 1, 1, 1)
-        quantize_tokens("mix", 1, 1, 1)
         turn("mix", 1, 1, 2)
         collect("mix", 1, 1, 2)
-        interleave(on_scalar, ("v", 1, 0, 0), 32, 64)
-        interleave(on_scalar, ("v", 1, 0, 1), 32, 64)
         interleave(on_scalar, ("v", 1, 0, 2), 32, 64)
-        quantize_tokens("mix", 1, 1, 2)
-        interleave(on_vector, ("v", 1, 0, 1), 0, 32)
-        quantize_rows(("v", 1, 0, 0))
+        interleave(on_scalar, ("v", 1, 1, 0), 32, 64)
         context(0, 1, 0)
         multiply(0, 1, 0)
+        quantize_rows(("v", 1, 0, 1))
         context(0, 1, 1)
         multiply(0, 1, 1)
-        quantize_rows(("v", 1, 0, 1))
-        context(0, 1, 2)
-        multiply(0, 1, 2)
-        context(0, 1, 3)
-        multiply(0, 1, 3)
+        quantize_rows(("v", 1, 0, 0))
         interleave(on_vector, ("v", 1, 0, 2), 0, 32)
-        interleave(on_vector, ("v", 1, 1, 0), 0, 48)
-        quantize_rows(("v", 1, 0, 2))
-        interleave(on_vector, ("v", 1, 1, 1), 0, 48)
         turn_back(0, 0, 0)
         collect_rows(on_scalar, 0, 0, 0)
         store_rows(0, 0, 0)
         turn_back(0, 0, 1)
         collect_rows(on_scalar, 0, 0, 1)
         store_rows(0, 0, 1)
+        context(0, 1, 2)
+        multiply(0, 1, 2)
+        context(0, 1, 3)
+        multiply(0, 1, 3)
+        quantize_tokens("mix", 1, 1, 0)
+        quantize_tokens("mix", 1, 1, 1)
+        quantize_tokens("mix", 1, 1, 2)
+        quantize_rows(("v", 1, 0, 2))
+        interleave(on_vector, ("v", 1, 1, 0), 0, 32)
+        interleave(on_vector, ("v", 1, 1, 1), 0, 64)
+        interleave(on_vector, ("v", 1, 1, 2), 0, 32)
+        quantize_rows(("v", 1, 1, 0))
         turn_back(0, 0, 2)
         collect_rows(on_scalar, 0, 0, 2)
         store_rows(0, 0, 2)
         turn_back(0, 0, 3)
         collect_rows(on_scalar, 0, 0, 3)
         store_rows(0, 0, 3)
-        interleave(on_scalar, ("v", 1, 1, 0), 48, 64)
-        quantize_rows(("v", 1, 1, 0))
-        interleave(on_vector, ("v", 1, 1, 2), 0, 48)
+        pre(1, 1, 0)
+        gate(1, 1, 0)
+        pre(1, 1, 1)
+        gate(1, 1, 1)
+        interleave(on_scalar, ("v", 1, 1, 2), 32, 64)
         turn_back(0, 1, 0)
         collect_rows(on_scalar, 0, 1, 0)
         store_rows(0, 1, 0)
         turn_back(0, 1, 1)
         collect_rows(on_scalar, 0, 1, 1)
         store_rows(0, 1, 1)
+        pre(1, 1, 2)
+        gate(1, 1, 2)
+        pre(1, 1, 3)
+        gate(1, 1, 3)
+        round_result(on_scalar, 0, 1, 48, 64)
+        context(1, 0, 0)
+        multiply(1, 0, 0)
+        quantize_rows(("v", 1, 1, 1))
+        context(1, 0, 1)
+        multiply(1, 0, 1)
+        quantize_rows(("v", 1, 1, 2))
         turn_back(0, 1, 2)
         collect_rows(on_scalar, 0, 1, 2)
         store_rows(0, 1, 2)
         turn_back(0, 1, 3)
         collect_rows(on_scalar, 0, 1, 3)
         store_rows(0, 1, 3)
-        interleave(on_scalar, ("v", 1, 1, 1), 48, 64)
-        interleave(on_scalar, ("v", 1, 1, 2), 48, 64)
         round_result(on_scalar, 0, 0, 0, 64)
-        quantize_rows(("v", 1, 1, 1))
-        context(1, 0, 0)
-        multiply(1, 0, 0)
-        quantize_rows(("v", 1, 1, 2))
-        context(1, 0, 1)
-        multiply(1, 0, 1)
         context(1, 0, 2)
         multiply(1, 0, 2)
         context(1, 0, 3)
         multiply(1, 0, 3)
-        quantize_result(0, 0)
-        store_words(0, 0)
-        round_result(on_vector, 0, 1, 0, 64)
-        pre(1, 1, 0)
-        gate(1, 1, 0)
-        pre(1, 1, 1)
-        gate(1, 1, 1)
-        pre(1, 1, 2)
-        gate(1, 1, 2)
-        pre(1, 1, 3)
-        gate(1, 1, 3)
+        round_result(on_vector, 0, 1, 0, 48)
         context(1, 1, 0)
         multiply(1, 1, 0)
+        quantize_result(0, 1)
         context(1, 1, 1)
         multiply(1, 1, 1)
-        quantize_result(0, 1)
-        round_result(on_vector, 1, 0, 0, 16)
+        quantize_result(0, 0)
         turn_back(1, 0, 0)
         collect_rows(on_scalar, 1, 0, 0)
         store_rows(1, 0, 0)
+        store_words(0, 1)
         turn_back(1, 0, 1)
         collect_rows(on_scalar, 1, 0, 1)
         store_rows(1, 0, 1)
+        store_words(0, 0)
         turn_back(1, 0, 2)
         collect_rows(on_scalar, 1, 0, 2)
         store_rows(1, 0, 2)
-        store_words(0, 1)
         turn_back(1, 0, 3)
         collect_rows(on_scalar, 1, 0, 3)
         store_rows(1, 0, 3)
-        round_result(on_scalar, 1, 0, 16, 64)
+        round_result(on_scalar, 1, 0, 40, 64)
         context(1, 1, 2)
         multiply(1, 1, 2)
         context(1, 1, 3)
         multiply(1, 1, 3)
+        round_result(on_vector, 1, 0, 0, 40)
         round_result(on_vector, 1, 1, 0, 64)
         quantize_result(1, 0)
         quantize_result(1, 1)
@@ -429,10 +454,10 @@ def tile_gated_cross_value_mix_g1_kernel(tc, mix, values, x, w_gate, b_gate, out
         turn_back(1, 1, 1)
         collect_rows(on_scalar, 1, 1, 1)
         store_rows(1, 1, 1)
-        store_words(1, 0)
         turn_back(1, 1, 2)
         collect_rows(on_scalar, 1, 1, 2)
         store_rows(1, 1, 2)
+        store_words(1, 0)
         store_words(1, 1)
         turn_back(1, 1, 3)
         collect_rows(on_scalar, 1, 1, 3)

@@ -50,7 +50,7 @@ def tile_gated_cross_value_mix_g1_kernel(tc, mix, values, x, w_gate, b_gate, out
             return codes[key], scales[key]
 
         def load_rows(key, src):
-            tile = sb.tile([P, PACK, GROUP], BF16, name="raw", bufs=10)
+            tile = sb.tile([P, PACK, GROUP], BF16, name="raw", bufs=4)
             nc.sync.dma_start(out=tile[:], in_=src.rearrange("(p j) n -> p j n", j=PACK))
             raw[key] = tile[:]
 
@@ -61,20 +61,27 @@ def tile_gated_cross_value_mix_g1_kernel(tc, mix, values, x, w_gate, b_gate, out
             load_rows(("v", b, g, c), values[b, K_PASS * c : K_PASS * (c + 1), GROUP * g : GROUP * (g + 1)])
 
         def load_v_wide(b, c):
-            tile = sb.tile([P, PACK, N], BF16, name="raw_wide", bufs=3)
+            tile = sb.tile([P, PACK, N], BF16, name="raw_wide", bufs=6)
             src = values[b, K_PASS * c : K_PASS * (c + 1), :]
             nc.sync.dma_start(out=tile[:], in_=src.rearrange("(p j) n -> p j n", j=PACK))
             for g in range(2):
                 raw[("v", b, g, c)] = tile[:, :, GROUP * g : GROUP * (g + 1)]
 
+        def load_w_wide(c):
+            tile = sb.tile([P, PACK, N], BF16, name="raw_wide", bufs=6)
+            src = w_gate[K_PASS * c : K_PASS * (c + 1), :]
+            nc.sync.dma_start(out=tile[:], in_=src.rearrange("(p j) n -> p j n", j=PACK))
+            for g in range(2):
+                raw[("w", g, c)] = tile[:, :, GROUP * g : GROUP * (g + 1)]
+
         def load_x(b, h):
-            tile = sb.tile([P, 2, D], BF16, name="raw", bufs=10)
-            nc.sync.dma_start(out=tile[:], in_=x[b, HALF * h : HALF * (h + 1), :].rearrange("(j p) k -> p j k", p=P))
+            tile = sb.tile([P, 2, D], BF16, name="raw", bufs=4)
+            nc.sync.dma_start(out=tile[:], in_=x[b, HALF * h : HALF * (h + 1), :].rearrange("(p j) k -> p j k", j=2))
             raw[("x", b, h)] = tile[:]
 
         def load_mix(b, h):
             tile = sb.tile([P, 2, S], BF16, name="raw_mix", bufs=3)
-            nc.sync.dma_start(out=tile[:], in_=mix[b, HALF * h : HALF * (h + 1), :].rearrange("(j p) k -> p j k", p=P))
+            nc.sync.dma_start(out=tile[:], in_=mix[b, HALF * h : HALF * (h + 1), :].rearrange("(p j) k -> p j k", j=2))
             raw[("mix", b, h)] = tile[:]
 
         def staging(key):
@@ -107,8 +114,8 @@ def tile_gated_cross_value_mix_g1_kernel(tc, mix, values, x, w_gate, b_gate, out
             tile = sb.tile([P, PACK * HALF], BF16, name="staged_tokens", bufs=6, align_bytes=64)
             staged[(name, b, h, c)] = tile
             nc.scalar.copy(
-                out=tile[:].bitcast(F32).rearrange("p (j r u) -> p j r u", j=2, u=2),
-                in_=bank[:].rearrange("p (j u r) -> p j r u", j=2, u=2),
+                out=tile[:].bitcast(F32).rearrange("p (r q) -> p r q", q=4),
+                in_=bank[:].rearrange("p (q r) -> p r q", q=4),
             )
 
         def quantize_tokens(name, b, h, c):
@@ -216,169 +223,162 @@ def tile_gated_cross_value_mix_g1_kernel(tc, mix, values, x, w_gate, b_gate, out
         nc.gpsimd.memset(warm[:, 0:1], 0.0)
         nc.scalar.activation(out=warm[:, 1:2], in_=warm[:, 0:1], func=TANH)
 
-        load_w(0, 0)
+        load_w_wide(0)
         load_x(0, 0)
-        load_w(0, 1)
         load_x(0, 1)
-        load_w(1, 0)
-        load_x(1, 0)
-        load_w(1, 1)
+        load_w_wide(1)
         nc.sync.dma_start(out=bias[:], in_=b_gate.rearrange("(g p t) -> p g t", g=2, t=PACK))
-        load_x(1, 1)
-        load_v(0, 0, 0)
-        load_v(0, 0, 1)
         load_mix(0, 0)
-        interleave(on_vector, ("w", 0, 0), 0, 64)
-        load_v(0, 0, 2)
+        load_v_wide(0, 0)
         load_mix(0, 1)
+        load_v_wide(0, 1)
+        load_x(1, 0)
+        load_x(1, 1)
+        load_mix(1, 0)
+        load_v_wide(0, 2)
+        load_v_wide(1, 0)
+        interleave(on_scalar, ("w", 0, 0), 32, 64)
+        interleave(on_vector, ("w", 0, 0), 0, 32)
+        interleave(on_vector, ("w", 1, 0), 0, 64)
+        load_v_wide(1, 1)
         quantize_rows(("w", 0, 0))
-        interleave(on_vector, ("w", 0, 1), 0, 64)
+        quantize_rows(("w", 1, 0))
         turn("x", 0, 0, 0)
         collect("x", 0, 0, 0)
         quantize_tokens("x", 0, 0, 0)
         turn("x", 0, 0, 1)
-        load_v(0, 1, 0)
-        load_v(0, 1, 1)
         collect("x", 0, 0, 1)
         quantize_tokens("x", 0, 0, 1)
-        quantize_rows(("w", 0, 1))
-        interleave(on_vector, ("w", 1, 0), 0, 48)
-        warm_up(2)
+        interleave(on_vector, ("w", 0, 1), 0, 32)
         turn("x", 0, 1, 0)
         collect("x", 0, 1, 0)
+        interleave(on_scalar, ("w", 0, 1), 32, 64)
         quantize_tokens("x", 0, 1, 0)
-        turn("x", 0, 1, 1)
-        load_v(0, 1, 2)
-        load_mix(1, 0)
-        collect("x", 0, 1, 1)
-        interleave(on_scalar, ("w", 1, 0), 48, 64)
-        quantize_tokens("x", 0, 1, 1)
-        interleave(on_vector, ("w", 1, 1), 0, 64)
-        quantize_rows(("w", 1, 0))
         warm_up(2)
+        turn("x", 0, 1, 1)
+        collect("x", 0, 1, 1)
+        interleave(on_scalar, ("w", 1, 1), 32, 64)
+        quantize_tokens("x", 0, 1, 1)
+        quantize_rows(("w", 0, 1))
+        interleave(on_vector, ("w", 1, 1), 0, 32)
+        warm_up(2)
+        turn("mix", 0, 0, 0)
+        collect("mix", 0, 0, 0)
+        quantize_tokens("mix", 0, 0, 0)
+        quantize_rows(("w", 1, 1))
+        interleave(on_vector, ("v", 0, 0, 0), 0, 64)
+        interleave(on_vector, ("v", 0, 1, 0), 0, 64)
+        turn("mix", 0, 0, 1)
+        collect("mix", 0, 0, 1)
+        quantize_tokens("mix", 0, 0, 1)
+        pre(0, 0, 0)
+        gate(0, 0, 0)
+        pre(0, 0, 1)
+        gate(0, 0, 1)
+        turn("mix", 0, 0, 2)
+        load_mix(1, 1)
+        load_v_wide(1, 2)
+        collect("mix", 0, 0, 2)
+        quantize_tokens("mix", 0, 0, 2)
+        quantize_rows(("v", 0, 0, 0))
+        interleave(on_vector, ("v", 0, 0, 1), 0, 64)
+        quantize_rows(("v", 0, 1, 0))
+        pre(0, 0, 2)
+        gate(0, 0, 2)
+        pre(0, 0, 3)
+        gate(0, 0, 3)
+        turn("mix", 0, 1, 0)
+        collect("mix", 0, 1, 0)
+        quantize_tokens("mix", 0, 1, 0)
+        turn("mix", 0, 1, 1)
+        collect("mix", 0, 1, 1)
+        quantize_tokens("mix", 0, 1, 1)
+        pre(0, 1, 0)
+        gate(0, 1, 0)
+        pre(0, 1, 1)
+        gate(0, 1, 1)
+        turn("mix", 0, 1, 2)
+        collect("mix", 0, 1, 2)
+        quantize_tokens("mix", 0, 1, 2)
+        interleave(on_vector, ("v", 0, 1, 1), 0, 64)
+        quantize_rows(("v", 0, 0, 1))
+        pre(0, 1, 2)
+        gate(0, 1, 2)
         turn("x", 1, 0, 0)
         collect("x", 1, 0, 0)
         quantize_tokens("x", 1, 0, 0)
         turn("x", 1, 0, 1)
         collect("x", 1, 0, 1)
         quantize_tokens("x", 1, 0, 1)
-        quantize_rows(("w", 1, 1))
-        interleave(on_vector, ("v", 0, 0, 0), 0, 64)
-        interleave(on_vector, ("v", 0, 0, 1), 0, 64)
-        pre(0, 0, 0)
-        gate(0, 0, 0)
-        pre(0, 0, 1)
-        gate(0, 0, 1)
-        pre(0, 0, 2)
-        gate(0, 0, 2)
-        pre(0, 0, 3)
-        gate(0, 0, 3)
+        pre(0, 1, 3)
+        gate(0, 1, 3)
         turn("x", 1, 1, 0)
         collect("x", 1, 1, 0)
         quantize_tokens("x", 1, 1, 0)
         turn("x", 1, 1, 1)
         collect("x", 1, 1, 1)
+        interleave(on_scalar, ("v", 0, 1, 2), 32, 64)
         quantize_tokens("x", 1, 1, 1)
-        quantize_rows(("v", 0, 0, 0))
         interleave(on_vector, ("v", 0, 0, 2), 0, 64)
-        quantize_rows(("v", 0, 0, 1))
-        pre(0, 1, 0)
-        gate(0, 1, 0)
-        pre(0, 1, 1)
-        gate(0, 1, 1)
-        turn("mix", 0, 0, 0)
-        collect("mix", 0, 0, 0)
-        quantize_tokens("mix", 0, 0, 0)
-        turn("mix", 0, 0, 1)
-        collect("mix", 0, 0, 1)
-        quantize_tokens("mix", 0, 0, 1)
-        pre(0, 1, 2)
-        gate(0, 1, 2)
-        pre(0, 1, 3)
-        gate(0, 1, 3)
-        turn("mix", 0, 0, 2)
-        load_mix(1, 1)
-        load_v_wide(1, 0)
-        load_v_wide(1, 1)
-        load_v_wide(1, 2)
-        collect("mix", 0, 0, 2)
-        quantize_tokens("mix", 0, 0, 2)
+        quantize_rows(("v", 0, 1, 1))
         quantize_rows(("v", 0, 0, 2))
-        interleave(on_vector, ("v", 0, 1, 0), 0, 64)
-        turn("mix", 0, 1, 0)
-        collect("mix", 0, 1, 0)
-        quantize_tokens("mix", 0, 1, 0)
+        interleave(on_vector, ("v", 0, 1, 2), 0, 32)
+        context_pass(0, 0, 0)
+        turn("mix", 1, 0, 0)
+        collect("mix", 1, 0, 0)
+        quantize_tokens("mix", 1, 0, 0)
+        turn("mix", 1, 0, 1)
+        collect("mix", 1, 0, 1)
+        quantize_tokens("mix", 1, 0, 1)
+        quantize_rows(("v", 0, 1, 2))
         pre(1, 0, 0)
         gate(1, 0, 0)
         pre(1, 0, 1)
         gate(1, 0, 1)
-        turn("mix", 0, 1, 1)
-        collect("mix", 0, 1, 1)
-        quantize_tokens("mix", 0, 1, 1)
-        turn("mix", 0, 1, 2)
-        collect("mix", 0, 1, 2)
-        quantize_tokens("mix", 0, 1, 2)
-        interleave(on_vector, ("v", 0, 1, 2), 0, 64)
-        quantize_rows(("v", 0, 1, 0))
+        interleave(on_scalar, ("v", 1, 0, 0), 0, 64)
+        context_pass(0, 0, 1)
         pre(1, 0, 2)
         gate(1, 0, 2)
         pre(1, 0, 3)
         gate(1, 0, 3)
-        interleave(on_scalar, ("v", 0, 1, 1), 0, 64)
-        context(0, 0, 0)
+        context_pass(0, 0, 2)
         multiply(0, 0, 0)
-        context(0, 0, 1)
         multiply(0, 0, 1)
-        quantize_rows(("v", 0, 1, 2))
-        quantize_rows(("v", 0, 1, 1))
-        turn("mix", 1, 0, 0)
-        collect("mix", 1, 0, 0)
-        turn("mix", 1, 0, 1)
-        collect("mix", 1, 0, 1)
-        context(0, 0, 2)
+        interleave(on_vector, ("v", 1, 0, 1), 0, 64)
         multiply(0, 0, 2)
+        multiply(0, 0, 3)
+        quantize_rows(("v", 1, 0, 1))
         turn("mix", 1, 0, 2)
         collect("mix", 1, 0, 2)
         turn("mix", 1, 1, 0)
         collect("mix", 1, 1, 0)
-        interleave(on_scalar, ("v", 1, 0, 0), 0, 64)
-        context(0, 0, 3)
-        multiply(0, 0, 3)
-        interleave(on_vector, ("v", 1, 0, 1), 0, 64)
-        quantize_tokens("mix", 1, 0, 0)
-        quantize_tokens("mix", 1, 0, 1)
+        interleave(on_scalar, ("v", 1, 0, 2), 0, 64)
+        context(0, 1, 0)
+        multiply(0, 1, 0)
         quantize_tokens("mix", 1, 0, 2)
+        quantize_tokens("mix", 1, 1, 0)
+        context(0, 1, 1)
+        multiply(0, 1, 1)
+        quantize_rows(("v", 1, 0, 0))
         turn("mix", 1, 1, 1)
         collect("mix", 1, 1, 1)
         turn("mix", 1, 1, 2)
         collect("mix", 1, 1, 2)
-        interleave(on_scalar, ("v", 1, 0, 2), 32, 64)
-        interleave(on_scalar, ("v", 1, 1, 0), 32, 64)
-        context(0, 1, 0)
-        multiply(0, 1, 0)
-        quantize_rows(("v", 1, 0, 1))
-        context(0, 1, 1)
-        multiply(0, 1, 1)
-        quantize_rows(("v", 1, 0, 0))
-        interleave(on_vector, ("v", 1, 0, 2), 0, 32)
+        context(0, 1, 2)
+        multiply(0, 1, 2)
         turn_back(0, 0, 0)
         collect_rows(on_scalar, 0, 0, 0)
         store_rows(0, 0, 0)
         turn_back(0, 0, 1)
         collect_rows(on_scalar, 0, 0, 1)
         store_rows(0, 0, 1)
-        context(0, 1, 2)
-        multiply(0, 1, 2)
         context(0, 1, 3)
         multiply(0, 1, 3)
-        quantize_tokens("mix", 1, 1, 0)
         quantize_tokens("mix", 1, 1, 1)
         quantize_tokens("mix", 1, 1, 2)
         quantize_rows(("v", 1, 0, 2))
-        interleave(on_vector, ("v", 1, 1, 0), 0, 32)
+        interleave(on_vector, ("v", 1, 1, 0), 0, 64)
         interleave(on_vector, ("v", 1, 1, 1), 0, 64)
-        interleave(on_vector, ("v", 1, 1, 2), 0, 32)
-        quantize_rows(("v", 1, 1, 0))
         turn_back(0, 0, 2)
         collect_rows(on_scalar, 0, 0, 2)
         store_rows(0, 0, 2)
@@ -389,7 +389,6 @@ def tile_gated_cross_value_mix_g1_kernel(tc, mix, values, x, w_gate, b_gate, out
         gate(1, 1, 0)
         pre(1, 1, 1)
         gate(1, 1, 1)
-        interleave(on_scalar, ("v", 1, 1, 2), 32, 64)
         turn_back(0, 1, 0)
         collect_rows(on_scalar, 0, 1, 0)
         store_rows(0, 1, 0)
@@ -400,13 +399,15 @@ def tile_gated_cross_value_mix_g1_kernel(tc, mix, values, x, w_gate, b_gate, out
         gate(1, 1, 2)
         pre(1, 1, 3)
         gate(1, 1, 3)
-        round_result(on_scalar, 0, 1, 48, 64)
+        interleave(on_scalar, ("v", 1, 1, 2), 32, 64)
+        quantize_rows(("v", 1, 1, 0))
+        interleave(on_vector, ("v", 1, 1, 2), 0, 32)
+        quantize_rows(("v", 1, 1, 1))
         context(1, 0, 0)
         multiply(1, 0, 0)
-        quantize_rows(("v", 1, 1, 1))
+        quantize_rows(("v", 1, 1, 2))
         context(1, 0, 1)
         multiply(1, 0, 1)
-        quantize_rows(("v", 1, 1, 2))
         turn_back(0, 1, 2)
         collect_rows(on_scalar, 0, 1, 2)
         store_rows(0, 1, 2)
@@ -418,7 +419,7 @@ def tile_gated_cross_value_mix_g1_kernel(tc, mix, values, x, w_gate, b_gate, out
         multiply(1, 0, 2)
         context(1, 0, 3)
         multiply(1, 0, 3)
-        round_result(on_vector, 0, 1, 0, 48)
+        round_result(on_vector, 0, 1, 0, 64)
         context(1, 1, 0)
         multiply(1, 1, 0)
         quantize_result(0, 1)
@@ -428,23 +429,23 @@ def tile_gated_cross_value_mix_g1_kernel(tc, mix, values, x, w_gate, b_gate, out
         turn_back(1, 0, 0)
         collect_rows(on_scalar, 1, 0, 0)
         store_rows(1, 0, 0)
-        store_words(0, 1)
         turn_back(1, 0, 1)
         collect_rows(on_scalar, 1, 0, 1)
         store_rows(1, 0, 1)
-        store_words(0, 0)
+        store_words(0, 1)
         turn_back(1, 0, 2)
         collect_rows(on_scalar, 1, 0, 2)
         store_rows(1, 0, 2)
+        store_words(0, 0)
         turn_back(1, 0, 3)
         collect_rows(on_scalar, 1, 0, 3)
         store_rows(1, 0, 3)
-        round_result(on_scalar, 1, 0, 40, 64)
+        round_result(on_scalar, 1, 0, 32, 64)
         context(1, 1, 2)
         multiply(1, 1, 2)
         context(1, 1, 3)
         multiply(1, 1, 3)
-        round_result(on_vector, 1, 0, 0, 40)
+        round_result(on_vector, 1, 0, 0, 32)
         round_result(on_vector, 1, 1, 0, 64)
         quantize_result(1, 0)
         quantize_result(1, 1)
@@ -454,10 +455,10 @@ def tile_gated_cross_value_mix_g1_kernel(tc, mix, values, x, w_gate, b_gate, out
         turn_back(1, 1, 1)
         collect_rows(on_scalar, 1, 1, 1)
         store_rows(1, 1, 1)
+        store_words(1, 0)
         turn_back(1, 1, 2)
         collect_rows(on_scalar, 1, 1, 2)
         store_rows(1, 1, 2)
-        store_words(1, 0)
         store_words(1, 1)
         turn_back(1, 1, 3)
         collect_rows(on_scalar, 1, 1, 3)

@@ -19,451 +19,373 @@ P = 128
 PACK = 4
 K_PASS = P * PACK
 GROUP = 512
-HALF = 256
-PAIRS = 64
+GROUPS = N // GROUP
+HALF_T = T // 2
+GATE_PASSES = D // K_PASS
+MIX_PASSES = S // K_PASS
+OPERANDS = (GROUPS + B) * GATE_PASSES + B * (GROUPS + 1) * MIX_PASSES
+LAST_OPERANDS = (("v", 1, 0, 2), ("v", 1, 1, 0), ("v", 1, 1, 1), ("v", 1, 1, 2))
+
+WHOLE = (0, 2)
+FIRST_PART = (0, 1)
+SECOND_PART = (1, 2)
 
 
 def tile_gated_cross_value_mix_g1_kernel(tc, mix, values, x, w_gate, b_gate, out_0, out_1, out_2):
     nc = tc.nc
+    on_vector = nc.vector.tensor_copy
+    on_scalar = nc.scalar.copy
+
     with ExitStack() as ctx:
         sb = ctx.enter_context(tc.tile_pool(name="sb", bufs=1))
-        psum = ctx.enter_context(tc.psum_pool(name="psum", bufs=8))
+        psum = ctx.enter_context(tc.psum_pool(name="psum", bufs=4))
         ctx.enter_context(tc.manual_schedule())
 
-        on_vector = nc.vector.tensor_copy
-        on_scalar = nc.scalar.copy
         raw = {}
         staged = {}
         codes = {}
         scales = {}
-        gated = {}
-        banks = {}
-        rows_out = {}
+        sums = {}
+        result = {}
+        rows = {}
+        words = {}
 
-        def new_bank(name):
-            return psum.tile([P, GROUP], F32, name=name, bufs=4)
+        def part_of(ap, part):
+            step = ap.shape[1] // 2
+            return ap[:, step * part[0] : step * part[1]]
 
-        def operand(key):
-            if key not in codes:
-                codes[key] = sb.tile([P, GROUP], U32, name="codes", bufs=22, align_bytes=64)
-                scales[key] = sb.tile([P, GROUP], U8, name="scales", bufs=22, align_bytes=64)
-            return codes[key], scales[key]
 
-        def load_rows(key, src):
-            tile = sb.tile([P, PACK, GROUP], BF16, name="raw", bufs=4)
-            nc.sync.dma_start(out=tile[:], in_=src.rearrange("(p j) n -> p j n", j=PACK))
-            raw[key] = tile[:]
+        def load_rows(name, src, c):
+            tile = sb.tile([P, PACK, N], BF16, name="raw_rows", bufs=6)
+            nc.sync.dma_start(out=tile[:], in_=src[K_PASS * c : K_PASS * (c + 1), :].rearrange("(p j) n -> p j n", j=PACK))
+            for g in range(GROUPS):
+                raw[name + (g, c)] = tile[:, :, GROUP * g : GROUP * (g + 1)]
 
-        def load_w(g, c):
-            load_rows(("w", g, c), w_gate[K_PASS * c : K_PASS * (c + 1), GROUP * g : GROUP * (g + 1)])
+        def load_w(c):
+            load_rows(("w",), w_gate, c)
 
-        def load_v(b, g, c):
-            load_rows(("v", b, g, c), values[b, K_PASS * c : K_PASS * (c + 1), GROUP * g : GROUP * (g + 1)])
+        def load_values(b, c):
+            load_rows(("v", b), values[b], c)
 
-        def load_v_wide(b, c):
-            tile = sb.tile([P, PACK, N], BF16, name="raw_wide", bufs=6)
-            src = values[b, K_PASS * c : K_PASS * (c + 1), :]
-            nc.sync.dma_start(out=tile[:], in_=src.rearrange("(p j) n -> p j n", j=PACK))
-            for g in range(2):
-                raw[("v", b, g, c)] = tile[:, :, GROUP * g : GROUP * (g + 1)]
-
-        def load_w_wide(c):
-            tile = sb.tile([P, PACK, N], BF16, name="raw_wide", bufs=6)
-            src = w_gate[K_PASS * c : K_PASS * (c + 1), :]
-            nc.sync.dma_start(out=tile[:], in_=src.rearrange("(p j) n -> p j n", j=PACK))
-            for g in range(2):
-                raw[("w", g, c)] = tile[:, :, GROUP * g : GROUP * (g + 1)]
+        def load_queries(name, src, b, h, bufs):
+            tile = sb.tile([P, 2, src.shape[2]], BF16, name="raw_" + name, bufs=bufs)
+            half = src[b, HALF_T * h : HALF_T * (h + 1), :]
+            nc.sync.dma_start(out=tile[:], in_=half.rearrange("(p e) k -> p e k", e=2))
+            raw[(name, b, h)] = tile[:]
 
         def load_x(b, h):
-            tile = sb.tile([P, 2, D], BF16, name="raw", bufs=4)
-            nc.sync.dma_start(out=tile[:], in_=x[b, HALF * h : HALF * (h + 1), :].rearrange("(p j) k -> p j k", j=2))
-            raw[("x", b, h)] = tile[:]
+            load_queries("x", x, b, h, bufs=4)
 
         def load_mix(b, h):
-            tile = sb.tile([P, 2, S], BF16, name="raw_mix", bufs=3)
-            nc.sync.dma_start(out=tile[:], in_=mix[b, HALF * h : HALF * (h + 1), :].rearrange("(p j) k -> p j k", j=2))
-            raw[("mix", b, h)] = tile[:]
+            load_queries("mix", mix, b, h, bufs=3)
 
-        def staging(key):
+
+        def operand_tiles(key):
+            if key not in codes:
+                reused = key[:2] in (("x", 0), ("w", 0)) or key in LAST_OPERANDS
+                tag, bufs = ("reused", len(LAST_OPERANDS)) if reused else ("kept", OPERANDS - 2 * len(LAST_OPERANDS))
+                codes[key] = sb.tile([P, GROUP], U32, name="codes_" + tag, bufs=bufs, align_bytes=64)
+                scales[key] = sb.tile([P, GROUP], U8, name="scales_" + tag, bufs=bufs, align_bytes=64)
+            return codes[key], scales[key]
+
+        def interleave(copy, key, part):
             if key not in staged:
-                staged[key] = sb.tile([P, PACK * GROUP], BF16, name="staged", bufs=5, align_bytes=64)
-            return staged[key]
-
-        def interleave(copy, key, lo, hi):
-            dst = staging(key)[:].rearrange("p (t a m j) -> p a t m j", t=PACK, m=2, j=PACK)
-            src = raw[key].rearrange("p j (a m t) -> p a t m j", m=2, t=PACK)
-            copy(out=dst[:, lo:hi], in_=src[:, lo:hi])
+                staged[key] = sb.tile([P, PACK * GROUP], BF16, name="staged_rows", bufs=5, align_bytes=64)
+            dst = staged[key][:].rearrange("p (t a i j) -> p a t i j", t=PACK, i=2, j=PACK)
+            src = raw[key].rearrange("p j (a i t) -> p a t i j", i=2, t=PACK)
+            copy(out=part_of(dst, part), in_=part_of(src, part))
 
         def quantize_rows(key):
-            cd, sc = operand(key)
+            cd, sc = operand_tiles(key)
             nc.vector.quantize_mx(out=cd[:].bitcast(FP8X4), scales=sc[:], in_=staged[key][:])
 
         def turn(name, b, h, c):
-            words = raw[(name, b, h)].bitcast(F32)
-            bank = new_bank("bank")
-            banks[(name, b, h, c)] = bank
-            for j in range(2):
+            pairs = raw[(name, b, h)].bitcast(F32)
+            pass_pairs = K_PASS // 2
+            bank = psum.tile([P, 2, 2, P], F32, name="bank")
+            for e in range(2):
                 for u in range(2):
-                    slot = 2 * j + u
-                    nc.tensor.transpose(
-                        bank[:, P * slot : P * (slot + 1)], words[:, j, 256 * c + u : 256 * (c + 1) : 2], ident[:]
-                    )
-
-        def collect(name, b, h, c):
-            bank = banks[(name, b, h, c)]
-            tile = sb.tile([P, PACK * HALF], BF16, name="staged_tokens", bufs=6, align_bytes=64)
+                    nc.tensor.transpose(bank[:, e, u, :], pairs[:, e, pass_pairs * c + u : pass_pairs * (c + 1) : 2], ident[:])
+            tile = sb.tile([P, PACK * HALF_T], BF16, name="staged_queries", bufs=6, align_bytes=64)
             staged[(name, b, h, c)] = tile
             nc.scalar.copy(
-                out=tile[:].bitcast(F32).rearrange("p (r q) -> p r q", q=4),
-                in_=bank[:].rearrange("p (q r) -> p r q", q=4),
+                out=tile[:].bitcast(F32).rearrange("p (r s) -> p r s", r=P),
+                in_=bank[:].rearrange("p e u r -> p r (e u)"),
             )
 
-        def quantize_tokens(name, b, h, c):
-            cd, sc = operand((name, b, c))
-            cols = slice(HALF * h, HALF * (h + 1))
+        def quantize_queries(name, b, h, c):
+            cd, sc = operand_tiles((name, b, c))
+            cols = slice(HALF_T * h, HALF_T * (h + 1))
             nc.vector.quantize_mx(out=cd[:, cols].bitcast(FP8X4), scales=sc[:, cols], in_=staged[(name, b, h, c)][:])
 
-        def product(name, stationary, moving, t):
-            bank = new_bank(name)
-            cols = slice(P * t, P * (t + 1))
-            for c in range(len(moving)):
-                nc.tensor.matmul_mx(
-                    out=bank[:],
-                    lhsT=codes[stationary[c]][:, cols].bitcast(FP8X4),
-                    lhsT_scale=scales[stationary[c]][:, cols],
-                    rhs=codes[moving[c]][:].bitcast(FP8X4),
-                    rhs_scale=scales[moving[c]][:],
-                    start=(c == 0),
-                    stop=(c == len(moving) - 1),
-                )
-            return bank
 
-        def pre(b, g, t):
-            banks[("pre", b, g, t)] = product("bank", [("w", g, c) for c in range(2)], [("x", b, c) for c in range(2)], t)
+        def mx_pass(bank, stationary, moving, t, c, passes):
+            cols = slice(P * t, P * (t + 1))
+            nc.tensor.matmul_mx(
+                out=bank[:],
+                lhsT=codes[stationary][:, cols].bitcast(FP8X4),
+                lhsT_scale=scales[stationary][:, cols],
+                rhs=codes[moving][:].bitcast(FP8X4),
+                rhs_scale=scales[moving][:],
+                start=(c == 0),
+                stop=(c == passes - 1),
+            )
+
+
+        def gate_pass(b, g, c):
+            for t in range(PACK):
+                if c == 0:
+                    sums[("pre", b, g, t)] = psum.tile([P, T], F32, name="sum")
+                mx_pass(sums[("pre", b, g, t)], ("w", g, c), ("x", b, c), t, c, GATE_PASSES)
+
+        def activate(b, g, t):
+            if (b, g) not in result:
+                result[(b, g)] = sb.tile([P, PACK, T], F32, name="result", bufs=B * GROUPS)
+            nc.scalar.activation(
+                out=result[(b, g)][:, t, :], in_=sums[("pre", b, g, t)][:], func=TANH, bias=bias[:, g, t : t + 1]
+            )
 
         def gate(b, g, t):
-            if (b, g) not in gated:
-                gated[(b, g)] = sb.tile([P, PACK, T], F32, name="gated", bufs=4)
-            bank = banks[("pre", b, g, t)]
-            nc.scalar.activation(out=gated[(b, g)][:, t, :], in_=bank[:], func=TANH, bias=bias[:, g, t : t + 1])
-
-        def context(b, g, t):
-            banks[(b, g, t)] = product("acc", [("v", b, g, c) for c in range(3)], [("mix", b, c) for c in range(3)], t)
+            sums[("pre", b, g, t)] = psum.tile([P, T], F32, name="bank")
+            for c in range(GATE_PASSES):
+                mx_pass(sums[("pre", b, g, t)], ("w", g, c), ("x", b, c), t, c, GATE_PASSES)
+            activate(b, g, t)
 
         def context_pass(b, g, c):
             for t in range(PACK):
                 if c == 0:
-                    banks[(b, g, t)] = new_bank("acc")
-                cols = slice(P * t, P * (t + 1))
-                nc.tensor.matmul_mx(
-                    out=banks[(b, g, t)][:],
-                    lhsT=codes[("v", b, g, c)][:, cols].bitcast(FP8X4),
-                    lhsT_scale=scales[("v", b, g, c)][:, cols],
-                    rhs=codes[("mix", b, c)][:].bitcast(FP8X4),
-                    rhs_scale=scales[("mix", b, c)][:],
-                    start=(c == 0),
-                    stop=(c == 2),
-                )
+                    sums[("context", b, g, t)] = psum.tile([P, T], F32, name="sum")
+                mx_pass(sums[("context", b, g, t)], ("v", b, g, c), ("mix", b, c), t, c, MIX_PASSES)
 
-        def warm_up(n):
-            bank = new_bank("acc")
-            key = ("w", 0, 0)
-            for i in range(n):
-                nc.tensor.matmul_mx(
-                    out=bank[:],
-                    lhsT=codes[key][:, :P].bitcast(FP8X4),
-                    lhsT_scale=scales[key][:, :P],
-                    rhs=codes[key][:].bitcast(FP8X4),
-                    rhs_scale=scales[key][:],
-                    start=True,
-                    stop=True,
-                )
+        def context(b, g, t):
+            sums[("context", b, g, t)] = psum.tile([P, T], F32, name="sum")
+            for c in range(MIX_PASSES):
+                mx_pass(sums[("context", b, g, t)], ("v", b, g, c), ("mix", b, c), t, c, MIX_PASSES)
 
         def multiply(b, g, t):
-            y_t = gated[(b, g)][:, t, :]
-            nc.vector.tensor_tensor(out=y_t, in0=banks[(b, g, t)][:], in1=y_t, op=MULT)
+            y_slot = result[(b, g)][:, t, :]
+            nc.vector.tensor_tensor(out=y_slot, in0=sums[("context", b, g, t)][:], in1=y_slot, op=MULT)
 
-        def turn_back(b, g, j):
-            bank = new_bank("bank")
-            banks[("back", b, g, j)] = bank
+
+        def turn_back(b, g, r):
+            bank = psum.tile([P, PACK, P], F32, name="bank")
             for t in range(PACK):
-                nc.tensor.transpose(bank[:, P * t : P * (t + 1)], gated[(b, g)][:, t, P * j : P * (j + 1)], ident[:])
+                nc.tensor.transpose(bank[:, t, :], result[(b, g)][:, t, P * r : P * (r + 1)], ident[:])
+            rows[(b, g, r)] = sb.tile([P, P, PACK], F32, name="rows", bufs=8)
+            nc.scalar.copy(out=rows[(b, g, r)][:], in_=bank[:].rearrange("p t m -> p m t"))
 
-        def collect_rows(copy, b, g, j):
-            bank = banks[("back", b, g, j)]
-            tile = sb.tile([P, GROUP], F32, name="rows_out", bufs=8)
-            copy(out=tile[:].rearrange("p (m t) -> p m t", t=PACK), in_=bank[:].rearrange("p (t m) -> p m t", t=PACK))
-            rows_out[(b, g, j)] = tile
+        def store_rows(b, g, r):
+            dst = out_0[b, P * r : P * (r + 1), GROUP * g : GROUP * (g + 1)]
+            nc.sync.dma_start(out=dst, in_=rows[(b, g, r)][:].rearrange("p m t -> p (m t)"))
 
-        def store_rows(b, g, j):
-            nc.sync.dma_start(out=out_0[b, P * j : P * (j + 1), GROUP * g : GROUP * (g + 1)], in_=rows_out[(b, g, j)][:])
-
-        def round_result(copy, b, g, lo, hi):
+        def round_result(copy, b, g, part):
             if ("y", b, g) not in staged:
-                staged[("y", b, g)] = sb.tile([P, PACK * GROUP], BF16, name="rounded", bufs=2, align_bytes=64)
-            dst = staged[("y", b, g)][:].rearrange("p (a i t) -> p a t i", i=4, t=PACK)
-            src = gated[(b, g)][:].rearrange("p t (a i) -> p a t i", i=4)
-            copy(out=dst[:, 2 * lo : 2 * hi], in_=src[:, 2 * lo : 2 * hi])
+                staged[("y", b, g)] = sb.tile([P, PACK * T], BF16, name="rounded", bufs=2, align_bytes=64)
+            dst = staged[("y", b, g)][:].rearrange("p (m t) -> p m t", t=PACK)
+            src = result[(b, g)][:].rearrange("p t m -> p m t")
+            copy(out=part_of(dst, part), in_=part_of(src, part))
 
         def quantize_result(b, g):
-            y_codes = sb.tile([P, T], U32, name="y_codes", bufs=4, align_bytes=64)
-            cols = slice(T * b, T * (b + 1))
-            nc.vector.quantize_mx(out=y_codes[:].bitcast(FP8X4), scales=y_scales[:, g, cols], in_=staged[("y", b, g)][:])
-            codes[("y", b, g)] = y_codes
+            words[(b, g)] = sb.tile([P, T], U32, name="y_words", bufs=B * GROUPS, align_bytes=64)
+            nc.vector.quantize_mx(
+                out=words[(b, g)][:].bitcast(FP8X4), scales=y_scales[:, g, T * b : T * (b + 1)], in_=staged[("y", b, g)][:]
+            )
 
         def store_words(b, g):
             dst = out_1[g].rearrange("p m t -> p (m t)").bitcast(I32)
-            nc.sync.dma_start(out=dst[:, T * b : T * (b + 1)], in_=codes[("y", b, g)][:].bitcast(I32))
+            nc.sync.dma_start(out=dst[:, T * b : T * (b + 1)], in_=words[(b, g)][:].bitcast(I32))
+
+        def store_scales(b):
+            cols = slice(T * b, T * (b + 1))
+            for q in range(4):
+                dst = out_2[:, 4 * q : 4 * (q + 1), cols].rearrange("g r m -> r g m")
+                nc.sync.dma_start(out=dst.bitcast(I32), in_=y_scales[32 * q : 32 * q + 4, :, cols].bitcast(I32))
+
 
         ident = sb.tile([P, P], F32, name="ident")
         make_identity(nc, ident[:])
-        bias = sb.tile([P, 2, PACK], BF16, name="bias")
-        y_scales = sb.tile([P, 2, B * T], U8, name="y_scales", align_bytes=64)
-        warm = sb.tile([P, 2], F32, name="warm")
-        nc.gpsimd.memset(warm[:, 0:1], 0.0)
-        nc.scalar.activation(out=warm[:, 1:2], in_=warm[:, 0:1], func=TANH)
+        bias = sb.tile([P, GROUPS, PACK], BF16, name="bias")
+        y_scales = sb.tile([P, GROUPS, B * T], U8, name="y_scales", align_bytes=64)
+        preload = sb.tile([P, 2], F32, name="preload")
+        nc.gpsimd.memset(preload[:, 0:1], 0.0)
+        nc.scalar.activation(out=preload[:, 1:2], in_=preload[:, 0:1], func=TANH)
 
-        load_w_wide(0)
+
+        load_w(0)
         load_x(0, 0)
         load_x(0, 1)
-        load_w_wide(1)
-        nc.sync.dma_start(out=bias[:], in_=b_gate.rearrange("(g p t) -> p g t", g=2, t=PACK))
-        load_mix(0, 0)
-        load_v_wide(0, 0)
-        load_mix(0, 1)
-        load_v_wide(0, 1)
+        load_w(1)
+        nc.sync.dma_start(out=bias[:], in_=b_gate.rearrange("(g p t) -> p g t", g=GROUPS, t=PACK))
+        for h in range(2):
+            load_mix(0, h)
+            load_values(0, h)
         load_x(1, 0)
         load_x(1, 1)
         load_mix(1, 0)
-        load_v_wide(0, 2)
-        load_v_wide(1, 0)
-        interleave(on_scalar, ("w", 0, 0), 32, 64)
-        interleave(on_vector, ("w", 0, 0), 0, 32)
-        interleave(on_vector, ("w", 1, 0), 0, 64)
-        load_v_wide(1, 1)
-        quantize_rows(("w", 0, 0))
-        quantize_rows(("w", 1, 0))
-        turn("x", 0, 0, 0)
-        collect("x", 0, 0, 0)
-        quantize_tokens("x", 0, 0, 0)
-        turn("x", 0, 0, 1)
-        collect("x", 0, 0, 1)
-        quantize_tokens("x", 0, 0, 1)
-        interleave(on_vector, ("w", 0, 1), 0, 32)
-        turn("x", 0, 1, 0)
-        collect("x", 0, 1, 0)
-        interleave(on_scalar, ("w", 0, 1), 32, 64)
-        quantize_tokens("x", 0, 1, 0)
-        warm_up(2)
-        turn("x", 0, 1, 1)
-        collect("x", 0, 1, 1)
-        interleave(on_scalar, ("w", 1, 1), 32, 64)
-        quantize_tokens("x", 0, 1, 1)
-        quantize_rows(("w", 0, 1))
-        interleave(on_vector, ("w", 1, 1), 0, 32)
-        warm_up(2)
+        load_values(0, 2)
+        load_values(1, 0)
+
+
+        interleave(on_vector, ("w", 0, 0), FIRST_PART)
+        interleave(on_scalar, ("w", 0, 0), SECOND_PART)
+        interleave(on_vector, ("w", 1, 0), WHOLE)
+        load_values(1, 1)
+        for g in range(GROUPS):
+            quantize_rows(("w", g, 0))
+        for h in range(2):
+            for c in range(GATE_PASSES):
+                turn("x", 0, h, c)
+                quantize_queries("x", 0, h, c)
+        for g in range(GROUPS):
+            interleave(on_vector, ("w", g, 1), FIRST_PART)
+            interleave(on_scalar, ("w", g, 1), SECOND_PART)
+        for g in range(GROUPS):
+            quantize_rows(("w", g, 1))
+
+
+        gate_pass(0, 0, 0)
         turn("mix", 0, 0, 0)
-        collect("mix", 0, 0, 0)
-        quantize_tokens("mix", 0, 0, 0)
-        quantize_rows(("w", 1, 1))
-        interleave(on_vector, ("v", 0, 0, 0), 0, 64)
-        interleave(on_vector, ("v", 0, 1, 0), 0, 64)
         turn("mix", 0, 0, 1)
-        collect("mix", 0, 0, 1)
-        quantize_tokens("mix", 0, 0, 1)
-        pre(0, 0, 0)
-        gate(0, 0, 0)
-        pre(0, 0, 1)
-        gate(0, 0, 1)
+        gate_pass(0, 0, 1)
+        interleave(on_vector, ("v", 0, 0, 0), WHOLE)
+        quantize_queries("mix", 0, 0, 0)
+        quantize_queries("mix", 0, 0, 1)
+        interleave(on_vector, ("v", 0, 1, 0), WHOLE)
+        quantize_rows(("v", 0, 0, 0))
+        activate(0, 0, 0)
+        activate(0, 0, 1)
         turn("mix", 0, 0, 2)
         load_mix(1, 1)
-        load_v_wide(1, 2)
-        collect("mix", 0, 0, 2)
-        quantize_tokens("mix", 0, 0, 2)
-        quantize_rows(("v", 0, 0, 0))
-        interleave(on_vector, ("v", 0, 0, 1), 0, 64)
+        load_values(1, 2)
+        activate(0, 0, 2)
+        activate(0, 0, 3)
+        quantize_queries("mix", 0, 0, 2)
         quantize_rows(("v", 0, 1, 0))
-        pre(0, 0, 2)
-        gate(0, 0, 2)
-        pre(0, 0, 3)
-        gate(0, 0, 3)
+        interleave(on_vector, ("v", 0, 0, 1), WHOLE)
         turn("mix", 0, 1, 0)
-        collect("mix", 0, 1, 0)
-        quantize_tokens("mix", 0, 1, 0)
-        turn("mix", 0, 1, 1)
-        collect("mix", 0, 1, 1)
-        quantize_tokens("mix", 0, 1, 1)
-        pre(0, 1, 0)
         gate(0, 1, 0)
-        pre(0, 1, 1)
         gate(0, 1, 1)
+        turn("mix", 0, 1, 1)
         turn("mix", 0, 1, 2)
-        collect("mix", 0, 1, 2)
-        quantize_tokens("mix", 0, 1, 2)
-        interleave(on_vector, ("v", 0, 1, 1), 0, 64)
+        for c in range(MIX_PASSES):
+            quantize_queries("mix", 0, 1, c)
+        interleave(on_vector, ("v", 0, 1, 1), WHOLE)
         quantize_rows(("v", 0, 0, 1))
-        pre(0, 1, 2)
-        gate(0, 1, 2)
-        turn("x", 1, 0, 0)
-        collect("x", 1, 0, 0)
-        quantize_tokens("x", 1, 0, 0)
-        turn("x", 1, 0, 1)
-        collect("x", 1, 0, 1)
-        quantize_tokens("x", 1, 0, 1)
-        pre(0, 1, 3)
-        gate(0, 1, 3)
-        turn("x", 1, 1, 0)
-        collect("x", 1, 1, 0)
-        quantize_tokens("x", 1, 1, 0)
-        turn("x", 1, 1, 1)
-        collect("x", 1, 1, 1)
-        interleave(on_scalar, ("v", 0, 1, 2), 32, 64)
-        quantize_tokens("x", 1, 1, 1)
-        interleave(on_vector, ("v", 0, 0, 2), 0, 64)
+        for h in range(2):
+            gate(0, 1, 2 + h)
+            for c in range(GATE_PASSES):
+                turn("x", 1, h, c)
+                quantize_queries("x", 1, h, c)
+
+
+        interleave(on_vector, ("v", 0, 0, 2), WHOLE)
         quantize_rows(("v", 0, 1, 1))
         quantize_rows(("v", 0, 0, 2))
-        interleave(on_vector, ("v", 0, 1, 2), 0, 32)
+        interleave(on_vector, ("v", 0, 1, 2), FIRST_PART)
+        interleave(on_scalar, ("v", 0, 1, 2), SECOND_PART)
         context_pass(0, 0, 0)
-        turn("mix", 1, 0, 0)
-        collect("mix", 1, 0, 0)
-        quantize_tokens("mix", 1, 0, 0)
-        turn("mix", 1, 0, 1)
-        collect("mix", 1, 0, 1)
-        quantize_tokens("mix", 1, 0, 1)
+        for c in range(2):
+            turn("mix", 1, 0, c)
+            quantize_queries("mix", 1, 0, c)
         quantize_rows(("v", 0, 1, 2))
-        pre(1, 0, 0)
         gate(1, 0, 0)
-        pre(1, 0, 1)
         gate(1, 0, 1)
-        interleave(on_scalar, ("v", 1, 0, 0), 0, 64)
         context_pass(0, 0, 1)
-        pre(1, 0, 2)
+        interleave(on_scalar, ("v", 1, 0, 0), WHOLE)
         gate(1, 0, 2)
-        pre(1, 0, 3)
         gate(1, 0, 3)
         context_pass(0, 0, 2)
+
+
         multiply(0, 0, 0)
         multiply(0, 0, 1)
-        interleave(on_vector, ("v", 1, 0, 1), 0, 64)
+        interleave(on_vector, ("v", 1, 0, 1), WHOLE)
         multiply(0, 0, 2)
         multiply(0, 0, 3)
         quantize_rows(("v", 1, 0, 1))
         turn("mix", 1, 0, 2)
-        collect("mix", 1, 0, 2)
         turn("mix", 1, 1, 0)
-        collect("mix", 1, 1, 0)
-        interleave(on_scalar, ("v", 1, 0, 2), 0, 64)
         context(0, 1, 0)
-        multiply(0, 1, 0)
-        quantize_tokens("mix", 1, 0, 2)
-        quantize_tokens("mix", 1, 1, 0)
         context(0, 1, 1)
+        interleave(on_scalar, ("v", 1, 0, 2), WHOLE)
+        multiply(0, 1, 0)
+        quantize_queries("mix", 1, 0, 2)
+        quantize_queries("mix", 1, 1, 0)
         multiply(0, 1, 1)
         quantize_rows(("v", 1, 0, 0))
         turn("mix", 1, 1, 1)
-        collect("mix", 1, 1, 1)
         turn("mix", 1, 1, 2)
-        collect("mix", 1, 1, 2)
-        context(0, 1, 2)
-        multiply(0, 1, 2)
-        turn_back(0, 0, 0)
-        collect_rows(on_scalar, 0, 0, 0)
-        store_rows(0, 0, 0)
-        turn_back(0, 0, 1)
-        collect_rows(on_scalar, 0, 0, 1)
-        store_rows(0, 0, 1)
-        context(0, 1, 3)
-        multiply(0, 1, 3)
-        quantize_tokens("mix", 1, 1, 1)
-        quantize_tokens("mix", 1, 1, 2)
+        for i in range(2):
+            context(0, 1, 2 + i)
+            multiply(0, 1, 2 + i)
+            for r in (2 * i, 2 * i + 1):
+                turn_back(0, 0, r)
+                store_rows(0, 0, r)
+        quantize_queries("mix", 1, 1, 1)
+        quantize_queries("mix", 1, 1, 2)
         quantize_rows(("v", 1, 0, 2))
-        interleave(on_vector, ("v", 1, 1, 0), 0, 64)
-        interleave(on_vector, ("v", 1, 1, 1), 0, 64)
-        turn_back(0, 0, 2)
-        collect_rows(on_scalar, 0, 0, 2)
-        store_rows(0, 0, 2)
-        turn_back(0, 0, 3)
-        collect_rows(on_scalar, 0, 0, 3)
-        store_rows(0, 0, 3)
-        pre(1, 1, 0)
-        gate(1, 1, 0)
-        pre(1, 1, 1)
-        gate(1, 1, 1)
-        turn_back(0, 1, 0)
-        collect_rows(on_scalar, 0, 1, 0)
-        store_rows(0, 1, 0)
-        turn_back(0, 1, 1)
-        collect_rows(on_scalar, 0, 1, 1)
-        store_rows(0, 1, 1)
-        pre(1, 1, 2)
-        gate(1, 1, 2)
-        pre(1, 1, 3)
-        gate(1, 1, 3)
-        interleave(on_scalar, ("v", 1, 1, 2), 32, 64)
+
+
+        interleave(on_vector, ("v", 1, 1, 0), WHOLE)
+        interleave(on_vector, ("v", 1, 1, 1), WHOLE)
         quantize_rows(("v", 1, 1, 0))
-        interleave(on_vector, ("v", 1, 1, 2), 0, 32)
+        interleave(on_vector, ("v", 1, 1, 2), FIRST_PART)
         quantize_rows(("v", 1, 1, 1))
+        gate(1, 1, 0)
+        gate(1, 1, 1)
+        for r in (0, 1):
+            turn_back(0, 1, r)
+            store_rows(0, 1, r)
+        gate(1, 1, 2)
+        gate(1, 1, 3)
         context(1, 0, 0)
+        context(1, 0, 1)
+        interleave(on_scalar, ("v", 1, 1, 2), SECOND_PART)
+        for r in (2, 3):
+            turn_back(0, 1, r)
+            store_rows(0, 1, r)
+        context(1, 0, 2)
+        context(1, 0, 3)
         multiply(1, 0, 0)
         quantize_rows(("v", 1, 1, 2))
-        context(1, 0, 1)
-        multiply(1, 0, 1)
-        turn_back(0, 1, 2)
-        collect_rows(on_scalar, 0, 1, 2)
-        store_rows(0, 1, 2)
-        turn_back(0, 1, 3)
-        collect_rows(on_scalar, 0, 1, 3)
-        store_rows(0, 1, 3)
-        round_result(on_scalar, 0, 0, 0, 64)
-        context(1, 0, 2)
-        multiply(1, 0, 2)
-        context(1, 0, 3)
-        multiply(1, 0, 3)
-        round_result(on_vector, 0, 1, 0, 64)
+        for t in range(1, PACK):
+            multiply(1, 0, t)
+
+
+        round_result(on_scalar, 0, 0, WHOLE)
+        round_result(on_vector, 0, 1, WHOLE)
         context(1, 1, 0)
+        context(1, 1, 1)
+        for r in range(PACK):
+            turn_back(1, 0, r)
+        context(1, 1, 2)
+        context(1, 1, 3)
         multiply(1, 1, 0)
         quantize_result(0, 1)
-        context(1, 1, 1)
         multiply(1, 1, 1)
         quantize_result(0, 0)
-        turn_back(1, 0, 0)
-        collect_rows(on_scalar, 1, 0, 0)
+        multiply(1, 1, 2)
+        multiply(1, 1, 3)
         store_rows(1, 0, 0)
-        turn_back(1, 0, 1)
-        collect_rows(on_scalar, 1, 0, 1)
         store_rows(1, 0, 1)
         store_words(0, 1)
-        turn_back(1, 0, 2)
-        collect_rows(on_scalar, 1, 0, 2)
         store_rows(1, 0, 2)
         store_words(0, 0)
-        turn_back(1, 0, 3)
-        collect_rows(on_scalar, 1, 0, 3)
+        store_scales(0)
         store_rows(1, 0, 3)
-        round_result(on_scalar, 1, 0, 32, 64)
-        context(1, 1, 2)
-        multiply(1, 1, 2)
-        context(1, 1, 3)
-        multiply(1, 1, 3)
-        round_result(on_vector, 1, 0, 0, 32)
-        round_result(on_vector, 1, 1, 0, 64)
-        quantize_result(1, 0)
-        quantize_result(1, 1)
-        turn_back(1, 1, 0)
-        collect_rows(on_scalar, 1, 1, 0)
+
+
+        round_result(on_vector, 1, 0, FIRST_PART)
+        round_result(on_scalar, 1, 0, SECOND_PART)
+        round_result(on_vector, 1, 1, WHOLE)
+        for g in range(GROUPS):
+            quantize_result(1, g)
+        for r in range(PACK):
+            turn_back(1, 1, r)
         store_rows(1, 1, 0)
-        turn_back(1, 1, 1)
-        collect_rows(on_scalar, 1, 1, 1)
         store_rows(1, 1, 1)
         store_words(1, 0)
-        turn_back(1, 1, 2)
-        collect_rows(on_scalar, 1, 1, 2)
         store_rows(1, 1, 2)
         store_words(1, 1)
-        turn_back(1, 1, 3)
-        collect_rows(on_scalar, 1, 1, 3)
+        store_scales(1)
         store_rows(1, 1, 3)
-
-        for q in range(4):
-            dst = out_2[:, 4 * q : 4 * (q + 1), :].rearrange("g r m -> r g m")
-            nc.sync.dma_start(out=dst.bitcast(I32), in_=y_scales[32 * q : 32 * q + 4, :, :].bitcast(I32))

@@ -54,6 +54,9 @@ def tile_gated_cross_value_mix_g1_kernel(tc, mix, values, x, w_gate, b_gate, out
             step = ap.shape[1] // 2
             return ap[:, step * part[0] : step * part[1]]
 
+        def half(h):
+            return slice(HALF_T * h, HALF_T * (h + 1))
+
 
         def load_rows(name, src, c):
             tile = sb.tile([P, PACK, N], BF16, name="raw_rows", bufs=6)
@@ -69,8 +72,7 @@ def tile_gated_cross_value_mix_g1_kernel(tc, mix, values, x, w_gate, b_gate, out
 
         def load_queries(name, src, b, h, bufs):
             tile = sb.tile([P, 2, src.shape[2]], BF16, name="raw_" + name, bufs=bufs)
-            half = src[b, HALF_T * h : HALF_T * (h + 1), :]
-            nc.sync.dma_start(out=tile[:], in_=half.rearrange("(p e) k -> p e k", e=2))
+            nc.sync.dma_start(out=tile[:], in_=src[b, half(h), :].rearrange("(p e) k -> p e k", e=2))
             raw[(name, b, h)] = tile[:]
 
         def load_x(b, h):
@@ -115,18 +117,17 @@ def tile_gated_cross_value_mix_g1_kernel(tc, mix, values, x, w_gate, b_gate, out
 
         def quantize_queries(name, b, h, c):
             cd, sc = operand_tiles((name, b, c))
-            cols = slice(HALF_T * h, HALF_T * (h + 1))
-            nc.vector.quantize_mx(out=cd[:, cols].bitcast(FP8X4), scales=sc[:, cols], in_=staged[(name, b, h, c)][:])
+            nc.vector.quantize_mx(out=cd[:, half(h)].bitcast(FP8X4), scales=sc[:, half(h)], in_=staged[(name, b, h, c)][:])
 
 
-        def mx_pass(bank, stationary, moving, t, c, passes):
+        def mx_pass(out, stationary, moving, t, c, passes, queries=slice(0, T)):
             cols = slice(P * t, P * (t + 1))
             nc.tensor.matmul_mx(
-                out=bank[:],
+                out=out,
                 lhsT=codes[stationary][:, cols].bitcast(FP8X4),
                 lhsT_scale=scales[stationary][:, cols],
-                rhs=codes[moving][:].bitcast(FP8X4),
-                rhs_scale=scales[moving][:],
+                rhs=codes[moving][:, queries].bitcast(FP8X4),
+                rhs_scale=scales[moving][:, queries],
                 start=(c == 0),
                 stop=(c == passes - 1),
             )
@@ -136,7 +137,7 @@ def tile_gated_cross_value_mix_g1_kernel(tc, mix, values, x, w_gate, b_gate, out
             for t in range(PACK):
                 if c == 0:
                     sums[("pre", b, g, t)] = psum.tile([P, T], F32, name="sum")
-                mx_pass(sums[("pre", b, g, t)], ("w", g, c), ("x", b, c), t, c, GATE_PASSES)
+                mx_pass(sums[("pre", b, g, t)][:], ("w", g, c), ("x", b, c), t, c, GATE_PASSES)
 
         def activate(b, g, t):
             if (b, g) not in result:
@@ -148,23 +149,34 @@ def tile_gated_cross_value_mix_g1_kernel(tc, mix, values, x, w_gate, b_gate, out
         def gate(b, g, t):
             sums[("pre", b, g, t)] = psum.tile([P, T], F32, name="bank")
             for c in range(GATE_PASSES):
-                mx_pass(sums[("pre", b, g, t)], ("w", g, c), ("x", b, c), t, c, GATE_PASSES)
+                mx_pass(sums[("pre", b, g, t)][:], ("w", g, c), ("x", b, c), t, c, GATE_PASSES)
             activate(b, g, t)
 
         def context_pass(b, g, c):
             for t in range(PACK):
                 if c == 0:
                     sums[("context", b, g, t)] = psum.tile([P, T], F32, name="sum")
-                mx_pass(sums[("context", b, g, t)], ("v", b, g, c), ("mix", b, c), t, c, MIX_PASSES)
+                mx_pass(sums[("context", b, g, t)][:], ("v", b, g, c), ("mix", b, c), t, c, MIX_PASSES)
 
         def context(b, g, t):
             sums[("context", b, g, t)] = psum.tile([P, T], F32, name="sum")
             for c in range(MIX_PASSES):
-                mx_pass(sums[("context", b, g, t)], ("v", b, g, c), ("mix", b, c), t, c, MIX_PASSES)
+                mx_pass(sums[("context", b, g, t)][:], ("v", b, g, c), ("mix", b, c), t, c, MIX_PASSES)
 
         def multiply(b, g, t):
             y_slot = result[(b, g)][:, t, :]
             nc.vector.tensor_tensor(out=y_slot, in0=sums[("context", b, g, t)][:], in1=y_slot, op=MULT)
+
+        def context_half(b, g, h, i):
+            bank = psum.tile([P, 2, HALF_T], F32, name="sum")
+            sums[("context", b, g, h, i)] = bank
+            for s in range(2):
+                for c in range(MIX_PASSES):
+                    mx_pass(bank[:, s, :], ("v", b, g, c), ("mix", b, c), 2 * i + s, c, MIX_PASSES, half(h))
+
+        def multiply_half(b, g, h, i):
+            y_part = result[(b, g)][:, 2 * i : 2 * i + 2, half(h)]
+            nc.vector.tensor_tensor(out=y_part, in0=sums[("context", b, g, h, i)][:], in1=y_part, op=MULT)
 
 
         def turn_back(b, g, r):
@@ -181,8 +193,8 @@ def tile_gated_cross_value_mix_g1_kernel(tc, mix, values, x, w_gate, b_gate, out
         def round_result(copy, b, g, part):
             if ("y", b, g) not in staged:
                 staged[("y", b, g)] = sb.tile([P, PACK * T], BF16, name="rounded", bufs=2, align_bytes=64)
-            dst = staged[("y", b, g)][:].rearrange("p (m t) -> p m t", t=PACK)
-            src = result[(b, g)][:].rearrange("p t m -> p m t")
+            dst = staged[("y", b, g)][:].rearrange("p (a i t) -> p a t i", i=4, t=PACK)
+            src = result[(b, g)][:].rearrange("p t (a i) -> p a t i", i=4)
             copy(out=part_of(dst, part), in_=part_of(src, part))
 
         def quantize_result(b, g):
@@ -329,7 +341,7 @@ def tile_gated_cross_value_mix_g1_kernel(tc, mix, values, x, w_gate, b_gate, out
         interleave(on_vector, ("v", 1, 1, 0), WHOLE)
         interleave(on_vector, ("v", 1, 1, 1), WHOLE)
         quantize_rows(("v", 1, 1, 0))
-        interleave(on_vector, ("v", 1, 1, 2), FIRST_PART)
+        interleave(on_vector, ("v", 1, 1, 2), WHOLE)
         quantize_rows(("v", 1, 1, 1))
         gate(1, 1, 0)
         gate(1, 1, 1)
@@ -340,7 +352,7 @@ def tile_gated_cross_value_mix_g1_kernel(tc, mix, values, x, w_gate, b_gate, out
         gate(1, 1, 3)
         context(1, 0, 0)
         context(1, 0, 1)
-        interleave(on_scalar, ("v", 1, 1, 2), SECOND_PART)
+        round_result(on_scalar, 0, 0, WHOLE)
         for r in (2, 3):
             turn_back(0, 1, r)
             store_rows(0, 1, r)
@@ -350,42 +362,42 @@ def tile_gated_cross_value_mix_g1_kernel(tc, mix, values, x, w_gate, b_gate, out
         quantize_rows(("v", 1, 1, 2))
         for t in range(1, PACK):
             multiply(1, 0, t)
+        quantize_result(0, 0)
+        store_words(0, 0)
+        round_result(on_scalar, 0, 1, SECOND_PART)
+        round_result(on_vector, 0, 1, FIRST_PART)
 
 
-        round_result(on_scalar, 0, 0, WHOLE)
-        round_result(on_vector, 0, 1, WHOLE)
-        context(1, 1, 0)
-        context(1, 1, 1)
+        context_half(1, 1, 0, 0)
+        context_half(1, 1, 0, 1)
         for r in range(PACK):
             turn_back(1, 0, r)
-        context(1, 1, 2)
-        context(1, 1, 3)
-        multiply(1, 1, 0)
+        context_half(1, 1, 1, 0)
+        context_half(1, 1, 1, 1)
+        multiply_half(1, 1, 0, 0)
         quantize_result(0, 1)
-        multiply(1, 1, 1)
-        quantize_result(0, 0)
-        multiply(1, 1, 2)
-        multiply(1, 1, 3)
+        multiply_half(1, 1, 0, 1)
         store_rows(1, 0, 0)
         store_rows(1, 0, 1)
         store_words(0, 1)
-        store_rows(1, 0, 2)
-        store_words(0, 0)
         store_scales(0)
+        store_rows(1, 0, 2)
         store_rows(1, 0, 3)
-
-
-        round_result(on_vector, 1, 0, FIRST_PART)
         round_result(on_scalar, 1, 0, SECOND_PART)
-        round_result(on_vector, 1, 1, WHOLE)
-        for g in range(GROUPS):
-            quantize_result(1, g)
-        for r in range(PACK):
-            turn_back(1, 1, r)
-        store_rows(1, 1, 0)
-        store_rows(1, 1, 1)
+        turn_back(1, 1, 0)
+        turn_back(1, 1, 1)
+        multiply_half(1, 1, 1, 0)
+        multiply_half(1, 1, 1, 1)
+        turn_back(1, 1, 2)
+        turn_back(1, 1, 3)
+        round_result(on_vector, 1, 0, FIRST_PART)
+        round_result(on_vector, 1, 1, FIRST_PART)
+        quantize_result(1, 0)
+        round_result(on_vector, 1, 1, SECOND_PART)
+        quantize_result(1, 1)
+        for r in range(3):
+            store_rows(1, 1, r)
         store_words(1, 0)
-        store_rows(1, 1, 2)
+        store_rows(1, 1, 3)
         store_words(1, 1)
         store_scales(1)
-        store_rows(1, 1, 3)

from contextlib import ExitStack

import concourse.mybir as mybir
from concourse.masks import make_identity

B, T, S, D, N = 2, 512, 1536, 1024, 1024
FLOPS = 2 * B * T * N * (S + D)

F32 = mybir.dt.float32
BF16 = mybir.dt.bfloat16
U32 = mybir.dt.uint32
I32 = mybir.dt.int32
U8 = mybir.dt.uint8
FP8X4 = mybir.dt.float8_e4m3fn_x4
TANH = mybir.ActivationFunctionType.Tanh
MULT = mybir.AluOpType.mult

P = 128
PACK = 4
K_PASS = P * PACK
GROUP = 512
GROUPS = N // GROUP
HALF_T = T // 2
GATE_PASSES = D // K_PASS
MIX_PASSES = S // K_PASS
OPERANDS = (GROUPS + B) * GATE_PASSES + B * (GROUPS + 1) * MIX_PASSES
LAST_OPERANDS = (("v", 1, 0, 2), ("v", 1, 1, 0), ("v", 1, 1, 1), ("v", 1, 1, 2))

WHOLE = (0, 2)
FIRST_PART = (0, 1)
SECOND_PART = (1, 2)


def tile_gated_cross_value_mix_g1_kernel(tc, mix, values, x, w_gate, b_gate, out_0, out_1, out_2):
    nc = tc.nc
    on_vector = nc.vector.tensor_copy
    on_scalar = nc.scalar.copy

    with ExitStack() as ctx:
        sb = ctx.enter_context(tc.tile_pool(name="sb", bufs=1))
        psum = ctx.enter_context(tc.psum_pool(name="psum", bufs=4))
        ctx.enter_context(tc.manual_schedule())

        raw = {}
        staged = {}
        codes = {}
        scales = {}
        sums = {}
        result = {}
        rows = {}
        words = {}

        def part_of(ap, part):
            step = ap.shape[1] // 2
            return ap[:, step * part[0] : step * part[1]]

        def half(h):
            return slice(HALF_T * h, HALF_T * (h + 1))


        def load_rows(name, src, c):
            tile = sb.tile([P, PACK, N], BF16, name="raw_rows", bufs=6)
            nc.sync.dma_start(out=tile[:], in_=src[K_PASS * c : K_PASS * (c + 1), :].rearrange("(p j) n -> p j n", j=PACK))
            for g in range(GROUPS):
                raw[name + (g, c)] = tile[:, :, GROUP * g : GROUP * (g + 1)]

        def load_w(c):
            load_rows(("w",), w_gate, c)

        def load_values(b, c):
            load_rows(("v", b), values[b], c)

        def load_queries(name, src, b, h, bufs):
            tile = sb.tile([P, 2, src.shape[2]], BF16, name="raw_" + name, bufs=bufs)
            nc.sync.dma_start(out=tile[:], in_=src[b, half(h), :].rearrange("(p e) k -> p e k", e=2))
            raw[(name, b, h)] = tile[:]

        def load_x(b, h):
            load_queries("x", x, b, h, bufs=4)

        def load_mix(b, h):
            load_queries("mix", mix, b, h, bufs=3)


        def operand_tiles(key):
            if key not in codes:
                reused = key[:2] in (("x", 0), ("w", 0)) or key in LAST_OPERANDS
                tag, bufs = ("reused", len(LAST_OPERANDS)) if reused else ("kept", OPERANDS - 2 * len(LAST_OPERANDS))
                codes[key] = sb.tile([P, GROUP], U32, name="codes_" + tag, bufs=bufs, align_bytes=64)
                scales[key] = sb.tile([P, GROUP], U8, name="scales_" + tag, bufs=bufs, align_bytes=64)
            return codes[key], scales[key]

        def interleave(copy, key, part):
            if key not in staged:
                staged[key] = sb.tile([P, PACK * GROUP], BF16, name="staged_rows", bufs=5, align_bytes=64)
            dst = staged[key][:].rearrange("p (t a i j) -> p a t i j", t=PACK, i=2, j=PACK)
            src = raw[key].rearrange("p j (a i t) -> p a t i j", i=2, t=PACK)
            copy(out=part_of(dst, part), in_=part_of(src, part))

        def quantize_rows(key):
            cd, sc = operand_tiles(key)
            nc.vector.quantize_mx(out=cd[:].bitcast(FP8X4), scales=sc[:], in_=staged[key][:])

        def turn(name, b, h, c):
            pairs = raw[(name, b, h)].bitcast(F32)
            pass_pairs = K_PASS // 2
            bank = psum.tile([P, 2, 2, P], F32, name="bank")
            for e in range(2):
                for u in range(2):
                    nc.tensor.transpose(bank[:, e, u, :], pairs[:, e, pass_pairs * c + u : pass_pairs * (c + 1) : 2], ident[:])
            tile = sb.tile([P, PACK * HALF_T], BF16, name="staged_queries", bufs=6, align_bytes=64)
            staged[(name, b, h, c)] = tile
            nc.scalar.copy(
                out=tile[:].bitcast(F32).rearrange("p (r s) -> p r s", r=P),
                in_=bank[:].rearrange("p e u r -> p r (e u)"),
            )

        def quantize_queries(name, b, h, c):
            cd, sc = operand_tiles((name, b, c))
            nc.vector.quantize_mx(out=cd[:, half(h)].bitcast(FP8X4), scales=sc[:, half(h)], in_=staged[(name, b, h, c)][:])


        def mx_pass(out, stationary, moving, t, c, passes, queries=slice(0, T)):
            cols = slice(P * t, P * (t + 1))
            nc.tensor.matmul_mx(
                out=out,
                lhsT=codes[stationary][:, cols].bitcast(FP8X4),
                lhsT_scale=scales[stationary][:, cols],
                rhs=codes[moving][:, queries].bitcast(FP8X4),
                rhs_scale=scales[moving][:, queries],
                start=(c == 0),
                stop=(c == passes - 1),
            )


        def gate_pass(b, g, c):
            for t in range(PACK):
                if c == 0:
                    sums[("pre", b, g, t)] = psum.tile([P, T], F32, name="sum")
                mx_pass(sums[("pre", b, g, t)][:], ("w", g, c), ("x", b, c), t, c, GATE_PASSES)

        def activate(b, g, t):
            if (b, g) not in result:
                result[(b, g)] = sb.tile([P, PACK, T], F32, name="result", bufs=B * GROUPS)
            nc.scalar.activation(
                out=result[(b, g)][:, t, :], in_=sums[("pre", b, g, t)][:], func=TANH, bias=bias[:, g, t : t + 1]
            )

        def gate(b, g, t):
            sums[("pre", b, g, t)] = psum.tile([P, T], F32, name="bank")
            for c in range(GATE_PASSES):
                mx_pass(sums[("pre", b, g, t)][:], ("w", g, c), ("x", b, c), t, c, GATE_PASSES)
            activate(b, g, t)

        def context_pass(b, g, c):
            for t in range(PACK):
                if c == 0:
                    sums[("context", b, g, t)] = psum.tile([P, T], F32, name="sum")
                mx_pass(sums[("context", b, g, t)][:], ("v", b, g, c), ("mix", b, c), t, c, MIX_PASSES)

        def context(b, g, t):
            sums[("context", b, g, t)] = psum.tile([P, T], F32, name="sum")
            for c in range(MIX_PASSES):
                mx_pass(sums[("context", b, g, t)][:], ("v", b, g, c), ("mix", b, c), t, c, MIX_PASSES)

        def multiply(b, g, t):
            y_slot = result[(b, g)][:, t, :]
            nc.vector.tensor_tensor(out=y_slot, in0=sums[("context", b, g, t)][:], in1=y_slot, op=MULT)

        def context_half(b, g, h, i):
            bank = psum.tile([P, 2, HALF_T], F32, name="sum")
            sums[("context", b, g, h, i)] = bank
            for s in range(2):
                for c in range(MIX_PASSES):
                    mx_pass(bank[:, s, :], ("v", b, g, c), ("mix", b, c), 2 * i + s, c, MIX_PASSES, half(h))

        def multiply_half(b, g, h, i):
            y_part = result[(b, g)][:, 2 * i : 2 * i + 2, half(h)]
            nc.vector.tensor_tensor(out=y_part, in0=sums[("context", b, g, h, i)][:], in1=y_part, op=MULT)


        def turn_back(b, g, r):
            bank = psum.tile([P, PACK, P], F32, name="bank")
            for t in range(PACK):
                nc.tensor.transpose(bank[:, t, :], result[(b, g)][:, t, P * r : P * (r + 1)], ident[:])
            rows[(b, g, r)] = sb.tile([P, P, PACK], F32, name="rows", bufs=8)
            nc.scalar.copy(out=rows[(b, g, r)][:], in_=bank[:].rearrange("p t m -> p m t"))

        def store_rows(b, g, r):
            dst = out_0[b, P * r : P * (r + 1), GROUP * g : GROUP * (g + 1)]
            nc.sync.dma_start(out=dst, in_=rows[(b, g, r)][:].rearrange("p m t -> p (m t)"))

        def round_result(copy, b, g, part):
            if ("y", b, g) not in staged:
                staged[("y", b, g)] = sb.tile([P, PACK * T], BF16, name="rounded", bufs=2, align_bytes=64)
            dst = staged[("y", b, g)][:].rearrange("p (a i t) -> p a t i", i=4, t=PACK)
            src = result[(b, g)][:].rearrange("p t (a i) -> p a t i", i=4)
            copy(out=part_of(dst, part), in_=part_of(src, part))

        def quantize_result(b, g):
            words[(b, g)] = sb.tile([P, T], U32, name="y_words", bufs=B * GROUPS, align_bytes=64)
            nc.vector.quantize_mx(
                out=words[(b, g)][:].bitcast(FP8X4), scales=y_scales[:, g, T * b : T * (b + 1)], in_=staged[("y", b, g)][:]
            )

        def store_words(b, g):
            dst = out_1[g].rearrange("p m t -> p (m t)").bitcast(I32)
            nc.sync.dma_start(out=dst[:, T * b : T * (b + 1)], in_=words[(b, g)][:].bitcast(I32))

        def store_scales(b):
            cols = slice(T * b, T * (b + 1))
            for q in range(4):
                dst = out_2[:, 4 * q : 4 * (q + 1), cols].rearrange("g r m -> r g m")
                nc.sync.dma_start(out=dst.bitcast(I32), in_=y_scales[32 * q : 32 * q + 4, :, cols].bitcast(I32))


        ident = sb.tile([P, P], F32, name="ident")
        make_identity(nc, ident[:])
        bias = sb.tile([P, GROUPS, PACK], BF16, name="bias")
        y_scales = sb.tile([P, GROUPS, B * T], U8, name="y_scales", align_bytes=64)
        preload = sb.tile([P, 2], F32, name="preload")
        nc.gpsimd.memset(preload[:, 0:1], 0.0)
        nc.scalar.activation(out=preload[:, 1:2], in_=preload[:, 0:1], func=TANH)


        load_w(0)
        load_x(0, 0)
        load_x(0, 1)
        load_w(1)
        nc.sync.dma_start(out=bias[:], in_=b_gate.rearrange("(g p t) -> p g t", g=GROUPS, t=PACK))
        for h in range(2):
            load_mix(0, h)
            load_values(0, h)
        load_x(1, 0)
        load_x(1, 1)
        load_mix(1, 0)
        load_values(0, 2)
        load_values(1, 0)


        interleave(on_vector, ("w", 0, 0), FIRST_PART)
        interleave(on_scalar, ("w", 0, 0), SECOND_PART)
        interleave(on_vector, ("w", 1, 0), WHOLE)
        load_values(1, 1)
        for g in range(GROUPS):
            quantize_rows(("w", g, 0))
        for h in range(2):
            for c in range(GATE_PASSES):
                turn("x", 0, h, c)
                quantize_queries("x", 0, h, c)
        for g in range(GROUPS):
            interleave(on_vector, ("w", g, 1), FIRST_PART)
            interleave(on_scalar, ("w", g, 1), SECOND_PART)
        for g in range(GROUPS):
            quantize_rows(("w", g, 1))


        gate_pass(0, 0, 0)
        turn("mix", 0, 0, 0)
        turn("mix", 0, 0, 1)
        gate_pass(0, 0, 1)
        interleave(on_vector, ("v", 0, 0, 0), WHOLE)
        quantize_queries("mix", 0, 0, 0)
        quantize_queries("mix", 0, 0, 1)
        interleave(on_vector, ("v", 0, 1, 0), WHOLE)
        quantize_rows(("v", 0, 0, 0))
        activate(0, 0, 0)
        activate(0, 0, 1)
        turn("mix", 0, 0, 2)
        load_mix(1, 1)
        load_values(1, 2)
        activate(0, 0, 2)
        activate(0, 0, 3)
        quantize_queries("mix", 0, 0, 2)
        quantize_rows(("v", 0, 1, 0))
        interleave(on_vector, ("v", 0, 0, 1), WHOLE)
        turn("mix", 0, 1, 0)
        gate(0, 1, 0)
        gate(0, 1, 1)
        turn("mix", 0, 1, 1)
        turn("mix", 0, 1, 2)
        for c in range(MIX_PASSES):
            quantize_queries("mix", 0, 1, c)
        interleave(on_vector, ("v", 0, 1, 1), WHOLE)
        quantize_rows(("v", 0, 0, 1))
        for h in range(2):
            gate(0, 1, 2 + h)
            for c in range(GATE_PASSES):
                turn("x", 1, h, c)
                quantize_queries("x", 1, h, c)


        interleave(on_vector, ("v", 0, 0, 2), WHOLE)
        quantize_rows(("v", 0, 1, 1))
        quantize_rows(("v", 0, 0, 2))
        interleave(on_vector, ("v", 0, 1, 2), FIRST_PART)
        interleave(on_scalar, ("v", 0, 1, 2), SECOND_PART)
        context_pass(0, 0, 0)
        for c in range(2):
            turn("mix", 1, 0, c)
            quantize_queries("mix", 1, 0, c)
        quantize_rows(("v", 0, 1, 2))
        gate(1, 0, 0)
        gate(1, 0, 1)
        context_pass(0, 0, 1)
        interleave(on_scalar, ("v", 1, 0, 0), WHOLE)
        gate(1, 0, 2)
        gate(1, 0, 3)
        context_pass(0, 0, 2)


        multiply(0, 0, 0)
        multiply(0, 0, 1)
        interleave(on_vector, ("v", 1, 0, 1), WHOLE)
        multiply(0, 0, 2)
        multiply(0, 0, 3)
        quantize_rows(("v", 1, 0, 1))
        turn("mix", 1, 0, 2)
        turn("mix", 1, 1, 0)
        context(0, 1, 0)
        context(0, 1, 1)
        interleave(on_scalar, ("v", 1, 0, 2), WHOLE)
        multiply(0, 1, 0)
        quantize_queries("mix", 1, 0, 2)
        quantize_queries("mix", 1, 1, 0)
        multiply(0, 1, 1)
        quantize_rows(("v", 1, 0, 0))
        turn("mix", 1, 1, 1)
        turn("mix", 1, 1, 2)
        for i in range(2):
            context(0, 1, 2 + i)
            multiply(0, 1, 2 + i)
            for r in (2 * i, 2 * i + 1):
                turn_back(0, 0, r)
                store_rows(0, 0, r)
        quantize_queries("mix", 1, 1, 1)
        quantize_queries("mix", 1, 1, 2)
        quantize_rows(("v", 1, 0, 2))


        interleave(on_vector, ("v", 1, 1, 0), WHOLE)
        interleave(on_vector, ("v", 1, 1, 1), WHOLE)
        quantize_rows(("v", 1, 1, 0))
        interleave(on_vector, ("v", 1, 1, 2), WHOLE)
        quantize_rows(("v", 1, 1, 1))
        gate(1, 1, 0)
        gate(1, 1, 1)
        for r in (0, 1):
            turn_back(0, 1, r)
            store_rows(0, 1, r)
        gate(1, 1, 2)
        gate(1, 1, 3)
        context(1, 0, 0)
        context(1, 0, 1)
        round_result(on_scalar, 0, 0, WHOLE)
        for r in (2, 3):
            turn_back(0, 1, r)
            store_rows(0, 1, r)
        context(1, 0, 2)
        context(1, 0, 3)
        multiply(1, 0, 0)
        quantize_rows(("v", 1, 1, 2))
        for t in range(1, PACK):
            multiply(1, 0, t)
        quantize_result(0, 0)
        store_words(0, 0)
        round_result(on_scalar, 0, 1, SECOND_PART)
        round_result(on_vector, 0, 1, FIRST_PART)


        context_half(1, 1, 0, 0)
        context_half(1, 1, 0, 1)
        for r in range(PACK):
            turn_back(1, 0, r)
        context_half(1, 1, 1, 0)
        context_half(1, 1, 1, 1)
        multiply_half(1, 1, 0, 0)
        quantize_result(0, 1)
        multiply_half(1, 1, 0, 1)
        store_rows(1, 0, 0)
        store_rows(1, 0, 1)
        store_words(0, 1)
        store_scales(0)
        store_rows(1, 0, 2)
        store_rows(1, 0, 3)
        round_result(on_scalar, 1, 0, SECOND_PART)
        turn_back(1, 1, 0)
        turn_back(1, 1, 1)
        multiply_half(1, 1, 1, 0)
        multiply_half(1, 1, 1, 1)
        turn_back(1, 1, 2)
        turn_back(1, 1, 3)
        round_result(on_vector, 1, 0, FIRST_PART)
        round_result(on_vector, 1, 1, FIRST_PART)
        quantize_result(1, 0)
        round_result(on_vector, 1, 1, SECOND_PART)
        quantize_result(1, 1)
        for r in range(3):
            store_rows(1, 1, r)
        store_words(1, 0)
        store_rows(1, 1, 3)
        store_words(1, 1)
        store_scales(1)
